import numpy as np
import ml_dtypes


def mxq(x, axis, fmt="e4m3"):
    dtype, down = {"e4m3": (ml_dtypes.float8_e4m3fn, 7), "e5m2": (ml_dtypes.float8_e5m2, 14)}[fmt]
    v = np.moveaxis(np.asarray(x, np.float32).astype(ml_dtypes.bfloat16).astype(np.float64), axis, -1)
    blocks = v.reshape(v.shape[:-1] + (-1, 32))
    amax = np.abs(blocks).max(-1, keepdims=True)
    byte = np.maximum(np.where(amax > 0, np.frexp(amax)[1] - 1 + 127, 0) - down, 1)
    scale = np.exp2(byte - 127.0)
    codes = (blocks / scale).astype(np.float32).astype(dtype).astype(np.float64)
    return np.moveaxis((codes * scale).reshape(v.shape), -1, axis)


WIDE = False


def mx_kscale(k):
    if not WIDE:
        return np.ones(k)
    levels = np.array([30, -30])
    if k % 512:
        return np.exp2(np.random.permutation(np.resize(levels, k // 32))).repeat(32)
    a = np.empty((k // 512, 16))
    for p in range(k // 512):
        a[p, :8] = np.random.permutation(np.resize(levels, 8))
        for g in range(8):
            far = levels[np.abs(levels - a[p, g]) >= 10]
            a[p, g + 8] = far[np.random.randint(len(far))]
    return np.exp2(a.ravel()).repeat(32)


def f64(x):
    return np.asarray(x).astype(np.float64)


def striped8(idx):
    return np.concatenate([v.reshape(-1, 16).T for v in idx]).astype(np.uint16)


def unstriped8(offs):
    return np.stack([offs[16 * g:16 * g + 16].T.reshape(-1) for g in range(8)]).astype(np.int64)


E2M1 = np.array([0.0, 0.5, 1.0, 1.5, 2.0, 3.0, 4.0, 6.0, -0.0, -0.5, -1.0, -1.5, -2.0, -3.0, -4.0, -6.0])


def pack_weight(w, fmt):
    k, n = w.shape
    w = f64(np.asarray(w, np.float32).astype(ml_dtypes.bfloat16)).reshape(k // 32, 32, n)
    amax = np.abs(w).max(1)
    if fmt == "e4m3":
        byte = np.frexp(amax)[1] - 1 + 127 - 7
    else:
        mant, ex = np.frexp(amax / 6.0)
        byte = np.where(mant > 0.5, ex, ex - 1) + 127
    byte = np.clip(np.where(amax > 0, byte, 1), 1, 254)
    scaled = (w * np.exp2(127.0 - byte)[:, None, :]).reshape(k, n).astype(np.float32)
    by_word = np.ascontiguousarray(scaled.reshape(k // 512, 128, 4, n).transpose(0, 1, 3, 2))
    if fmt == "e4m3":
        words = by_word.astype(ml_dtypes.float8_e4m3fn).view(np.uint8)
    else:
        c = by_word.astype(ml_dtypes.float4_e2m1fn).view(np.uint8) & 0xF
        words = (c[..., 0::2] | (c[..., 1::2] << 4)).reshape(k // 512, 128, 2 * n)
    return np.ascontiguousarray(words), np.ascontiguousarray(byte.astype(np.uint8).reshape(k // 512, 16, n))


def unpack_weight(words, scales, fmt):
    g, _, n = scales.shape
    words = np.ascontiguousarray(words).reshape(g, 128, n, -1)
    if fmt == "e4m3":
        vals = words.view(ml_dtypes.float8_e4m3fn).astype(np.float64)
    else:
        nib = np.empty((g, 128, n, 4), np.uint8)
        nib[..., 0::2] = words & 0xF
        nib[..., 1::2] = words >> 4
        vals = E2M1[nib]
    vals = vals * np.repeat(np.exp2(scales.astype(np.float64) - 127.0), 8, axis=1)[..., None]
    return vals.transpose(0, 1, 3, 2).reshape(g * 512, n)


K, N, T, J = 1024, 1024, 2048, 1024


def setup_inputs():
    n = np.random.standard_normal
    s = mx_kscale(K)[:, None]
    m = np.exp(0.5 * n((1, J)))
    w = n((K, N)) / np.sqrt(K) / s
    p_w4 = pack_weight(w[512:], "e2m1")
    return {
        "dy": (m * n((K, J)) * s).astype(np.float32),
        "w8": (w[:512]).astype(np.float32),
        "w4_words": p_w4[0],
        "w4_scales": p_w4[1],
        "res": (n((N, J))).astype(np.float32),
        "wgo": np.repeat(np.random.uniform(0.5, 2.0, (8, J)), 16, axis=0).astype(np.float32),
        "offs": striped8(np.stack([np.random.permutation(T)[:J] for _ in range(8)])),
    }


def reference(dy, w8, w4_words, w4_scales, res, wgo, offs):
    idx = unstriped8(offs)
    dy_ = mxq(f64(dy), 0, "e5m2")
    w8_ = mxq(f64(w8), 0, "e4m3")
    w4_ = unpack_weight(w4_words, w4_scales, "e2m1")
    dx = w8_.T @ dy_[:512] + w4_.T @ dy_[512:]
    out = np.zeros((N, T))
    rows = np.arange(N)
    out[rows[:, None], idx[rows % 128 // 16]] = f64(wgo)[rows % 128] * (dx + f64(res))
    return out

@@ -1,0 +1,200 @@
+from contextlib import ExitStack
+
+import concourse.mybir as mybir
+from concourse.masks import make_identity
+
+K, N, T, J = 1024, 1024, 2048, 1024
+FLOPS = 2 * K * N * J
+
+F32 = mybir.dt.float32
+BF16 = mybir.dt.bfloat16
+I32 = mybir.dt.int32
+U32 = mybir.dt.uint32
+U16 = mybir.dt.uint16
+U8 = mybir.dt.uint8
+E4M3 = mybir.dt.float8_e4m3fn_x4
+E5M2 = mybir.dt.float8_e5m2_x4
+E2M1 = mybir.dt.float4_e2m1fn_x4
+ADD = mybir.AluOpType.add
+MULT = mybir.AluOpType.mult
+
+P = 128
+PACK = 4
+K_PASS = P * PACK
+HALF = 512
+TILES = N // P
+WINDOWS = 4
+
+
+def tile_list_embg_qf_res_kernel(tc, dy, w8, w4_words, w4_scales, res, wgo, offs, out):
+    nc = tc.nc
+    with ExitStack() as ctx:
+        keep = ctx.enter_context(tc.tile_pool(name="keep", bufs=1))
+        ring = ctx.enter_context(tc.tile_pool(name="ring", bufs=3))
+        psum_mx = ctx.enter_context(tc.psum_pool(name="psum_mx", bufs=3))
+        psum_turn = ctx.enter_context(tc.psum_pool(name="psum_turn", bufs=3))
+        psum_back = ctx.enter_context(tc.psum_pool(name="psum_back", bufs=2))
+
+        offsets = keep.tile([P, J // 16], U16, name="offsets")
+        weight = keep.tile([P, J], F32, name="weight")
+        w4_codes = keep.tile([P, 2 * N], U8, name="w4_codes", align_bytes=64)
+        w4_plane = keep.tile([P, N], U8, name="w4_plane", align_bytes=64)
+        ident = keep.tile([P, P], F32, name="ident")
+        windows = [keep.tile([P, T], F32, name="window%d" % w) for w in range(2)]
+        sums = [keep.tile([P, J], F32, name="sum%d" % i) for i in range(TILES)]
+        dy_codes = {}
+        dy_plane = {}
+        for a in range(2):
+            for h in range(2):
+                dy_codes[a, h] = keep.tile([P, HALF], U32, name="dy_codes%d%d" % (a, h), align_bytes=64)
+                dy_plane[a, h] = keep.tile([P, HALF], U8, name="dy_plane%d%d" % (a, h), align_bytes=64)
+
+        def load_rows(name, rows):
+            raw = keep.tile([P, PACK, rows.shape[1]], F32, name=name)
+            nc.sync.dma_start(out=raw[:], in_=rows.rearrange("(p t) c -> p t c", t=PACK))
+            return raw
+
+        def load_res(i, count, c0, c1):
+            raw = keep.tile([P, count, c1 - c0], F32, name="res_%d_%d" % (i, c0), tag="res_%d_%d" % (i, c0), align_bytes=64)
+            nc.sync.dma_start(out=raw[:], in_=res[i * P : (i + count) * P, c0:c1].rearrange("(i p) c -> p i c", p=P))
+            for d in range(count):
+                for c in range(c0, c1, HALF):
+                    res_of[i + d, c // HALF] = raw[:, d, c - c0 : c - c0 + HALF]
+
+        def interleave(engine, name, raw, step):
+            width = raw.shape[2]
+            grouped = keep.tile([P, width * PACK], BF16, name=name, tag=name, align_bytes=64)
+            for c in range(0, width, step):
+                dst = grouped[:, c * PACK : (c + step) * PACK].rearrange("p (c i t) -> p c t i", i=4, t=PACK)
+                src = raw[:, :, c : c + step].rearrange("p t (c i) -> p c t i", i=4)
+                if engine == "vector":
+                    nc.vector.tensor_copy(out=dst, in_=src)
+                else:
+                    nc.scalar.copy(out=dst, in_=src)
+            return grouped
+
+        def quantize_w8(name, grouped, first_tile):
+            width = grouped.shape[1] // PACK
+            codes = keep.tile([P, width], U32, name=name + "_codes", align_bytes=64)
+            plane = keep.tile([P, width], U8, name=name + "_plane", align_bytes=64)
+            nc.vector.quantize_mx(out=codes[:].bitcast(E4M3), scales=plane[:], in_=grouped[:])
+            for d in range(width // P):
+                w8_of[first_tile + d] = (codes[:, d * P : (d + 1) * P], plane[:, d * P : (d + 1) * P])
+
+        def quantize_dy(grouped, a, h, c0):
+            cols = slice(c0, c0 + grouped.shape[1] // PACK)
+            nc.vector.quantize_mx(out=dy_codes[a, h][:, cols].bitcast(E5M2), scales=dy_plane[a, h][:, cols], in_=grouped[:])
+
+        def product(i, h):
+            acc = psum_mx.tile([P, HALF], F32, name="acc")
+            codes, plane = w8_of[i]
+            nc.tensor.matmul_mx(
+                out=acc[:], lhsT=codes.bitcast(E4M3), lhsT_scale=plane,
+                rhs=dy_codes[0, h][:].bitcast(E5M2), rhs_scale=dy_plane[0, h][:], start=True, stop=False,
+            )
+            nc.tensor.matmul_mx(
+                out=acc[:], lhsT=w4_codes[:, 2 * P * i : 2 * P * (i + 1)].bitcast(E2M1), lhsT_scale=w4_plane[:, P * i : P * (i + 1)],
+                rhs=dy_codes[1, h][:].bitcast(E5M2), rhs_scale=dy_plane[1, h][:], start=False, stop=True,
+            )
+            return acc
+
+        def sum_on_vector(i, h):
+            acc = product(i, h)
+            nc.vector.tensor_tensor(out=sums[i][:, h * HALF : (h + 1) * HALF], in0=acc[:], in1=res_of[i, h], op=ADD)
+
+        def sum_on_tensor(i, h):
+            blocks = [slice(b * P, (b + 1) * P) for b in range(HALF // P)]
+            turned = psum_turn.tile([P, HALF], F32, name="turned")
+            for b, cols in enumerate(blocks):
+                nc.tensor.matmul(turned[:, cols], res_of[i, h][:, cols], ident[:], start=(b == 0), stop=False, is_transpose=True)
+            acc = product(i, h)
+            dx = ring.tile([P, HALF], F32, name="dx")
+            nc.scalar.copy(out=dx[:], in_=acc[:])
+            for b, cols in enumerate(blocks):
+                nc.tensor.matmul(turned[:, cols], dx[:, cols], ident[:], start=False, stop=(b == len(blocks) - 1), is_transpose=True)
+            sum_t = ring.tile([P, HALF], F32, name="sum_t")
+            nc.scalar.copy(out=sum_t[:], in_=turned[:])
+            back = psum_back.tile([P, HALF], F32, name="back")
+            for cols in blocks:
+                nc.tensor.transpose(back[:, cols], sum_t[:, cols], ident[:])
+            nc.scalar.copy(out=sums[i][:, h * HALF : (h + 1) * HALF], in_=back[:])
+
+        def scatter(i, c0, c1):
+            nc.vector.tensor_tensor(
+                out=windows[i % WINDOWS][:].indirect(offsets[:, c0 // 16 : c1 // 16]),
+                in0=sums[i][:, c0:c1], in1=weight[:, c0:c1], op=MULT,
+            )
+
+        def store(i):
+            nc.sync.dma_start(out=out[i * P : (i + 1) * P, :], in_=windows[i % WINDOWS][:])
+
+        def late_window(tag):
+            window = keep.tile([P, T], F32, name="window%d" % len(windows), tag=tag, align_bytes=64)
+            nc.gpsimd.memset(window[:], 0.0)
+            windows.append(window)
+
+        res_of = {}
+        w8_of = {}
+
+        nc.vector.memset(w4_plane[:].bitcast(I32), 0)
+        make_identity(nc, ident[:])
+        for w in range(2):
+            nc.vector.memset(windows[w][:], 0.0)
+
+        raw_00 = load_rows("raw_00", dy[0:K_PASS, 0:HALF])
+        raw_wa = load_rows("raw_wa", w8[:, 0:256])
+        staged = keep.tile([P, N // 4], I32, name="staged")
+        for q in range(4):
+            rows = slice(32 * q, 32 * q + 4)
+            nc.sync.dma_start(out=staged[rows, :], in_=w4_scales[0, 4 * q : 4 * q + 4, :].bitcast(I32))
+            nc.vector.tensor_copy(out=w4_plane[:].bitcast(I32)[rows, :], in_=staged[rows, :])
+        raw_10a = load_rows("raw_10a", dy[K_PASS:K, 0:256])
+        raw_10b = load_rows("raw_10b", dy[K_PASS:K, 256:HALF])
+        nc.sync.dma_start(out=w4_codes[:].bitcast(I32), in_=w4_words[0].bitcast(I32))
+        load_res(0, 1, 0, HALF)
+        nc.sync.dma_start(offsets[:], offs)
+        nc.sync.dma_start(out=weight[:, 0:HALF], in_=wgo[:, 0:HALF])
+        load_res(1, 1, 0, HALF)
+        raw_wb = load_rows("raw_wb", w8[:, 256:512])
+        load_res(2, 1, 0, HALF)
+        raw_01 = load_rows("raw_01", dy[0:K_PASS, HALF:J])
+        raw_11 = load_rows("raw_11", dy[K_PASS:K, HALF:J])
+        load_res(3, 1, 0, HALF)
+        load_res(0, 2, HALF, J)
+        nc.sync.dma_start(out=weight[:, HALF:J], in_=wgo[:, HALF:J])
+        load_res(2, 2, HALF, J)
+        raw_wc = load_rows("raw_wc", w8[:, 512:N])
+        load_res(4, 2, 0, J)
+        load_res(6, 2, 0, J)
+
+        quantize_dy(interleave("vector", "g_00", raw_00, 512), 0, 0, 0)
+        quantize_w8("wa", interleave("scalar", "g_wa", raw_wa, 256), 0)
+        quantize_dy(interleave("vector", "g_10a", raw_10a, 256), 1, 0, 0)
+        quantize_dy(interleave("vector", "g_10b", raw_10b, 256), 1, 0, 256)
+
+        late_window("g_10b")
+        sum_on_vector(0, 0)
+        late_window("res_0_0")
+        scatter(0, 0, HALF)
+        sum_on_tensor(1, 0)
+        scatter(1, 0, HALF)
+        quantize_w8("wb", interleave("scalar", "g_wb", raw_wb, 256), 2)
+        sum_on_tensor(2, 0)
+        scatter(2, 0, HALF)
+        quantize_dy(interleave("scalar", "g_01", raw_01, 256), 0, 1, 0)
+        quantize_dy(interleave("scalar", "g_11", raw_11, 256), 1, 1, 0)
+        sum_on_tensor(3, 0)
+        scatter(3, 0, HALF)
+        sum_on_vector(0, 1)
+        scatter(0, HALF, J)
+        store(0)
+        quantize_w8("wc", interleave("scalar", "g_wc", raw_wc, 256), 4)
+        for i in range(1, 4):
+            sum_on_tensor(i, 1)
+            scatter(i, HALF, J)
+            store(i)
+        for i in range(4, TILES):
+            sum_on_tensor(i, 0)
+            sum_on_tensor(i, 1)
+            scatter(i, 0, J)
+            store(i)

@@ -31,8 +31,8 @@ def tile_list_embg_qf_res_kernel(tc, dy, w8, w4_words, w4_scales, res, wgo, offs
     with ExitStack() as ctx:
         keep = ctx.enter_context(tc.tile_pool(name="keep", bufs=1))
         ring = ctx.enter_context(tc.tile_pool(name="ring", bufs=3))
-        psum_mx = ctx.enter_context(tc.psum_pool(name="psum_mx", bufs=3))
-        psum_turn = ctx.enter_context(tc.psum_pool(name="psum_turn", bufs=3))
+        psum_mx = ctx.enter_context(tc.psum_pool(name="psum_mx", bufs=4))
+        psum_turn = ctx.enter_context(tc.psum_pool(name="psum_turn", bufs=2))
         psum_back = ctx.enter_context(tc.psum_pool(name="psum_back", bufs=2))
 
         offsets = keep.tile([P, J // 16], U16, name="offsets")
@@ -40,8 +40,8 @@ def tile_list_embg_qf_res_kernel(tc, dy, w8, w4_words, w4_scales, res, wgo, offs
         w4_codes = keep.tile([P, 2 * N], U8, name="w4_codes", align_bytes=64)
         w4_plane = keep.tile([P, N], U8, name="w4_plane", align_bytes=64)
         ident = keep.tile([P, P], F32, name="ident")
-        windows = [keep.tile([P, T], F32, name="window%d" % w) for w in range(2)]
-        sums = [keep.tile([P, J], F32, name="sum%d" % i) for i in range(TILES)]
+        windows = [keep.tile([P, T], F32, name="window%d" % w) for w in range(WINDOWS)]
+        sums = {}
         dy_codes = {}
         dy_plane = {}
         for a in range(2):
@@ -61,16 +61,19 @@ def tile_list_embg_qf_res_kernel(tc, dy, w8, w4_words, w4_scales, res, wgo, offs
                 for c in range(c0, c1, HALF):
                     res_of[i + d, c // HALF] = raw[:, d, c - c0 : c - c0 + HALF]
 
-        def interleave(engine, name, raw, step):
-            width = raw.shape[2]
+        def interleave(engine, name, raws, step):
+            width = sum(raw.shape[2] for raw in raws)
             grouped = keep.tile([P, width * PACK], BF16, name=name, tag=name, align_bytes=64)
-            for c in range(0, width, step):
-                dst = grouped[:, c * PACK : (c + step) * PACK].rearrange("p (c i t) -> p c t i", i=4, t=PACK)
-                src = raw[:, :, c : c + step].rearrange("p t (c i) -> p c t i", i=4)
-                if engine == "vector":
-                    nc.vector.tensor_copy(out=dst, in_=src)
-                else:
-                    nc.scalar.copy(out=dst, in_=src)
+            at = 0
+            for raw in raws:
+                for c in range(0, raw.shape[2], step):
+                    dst = grouped[:, at * PACK : (at + step) * PACK].rearrange("p (c i t) -> p c t i", i=4, t=PACK)
+                    src = raw[:, :, c : c + step].rearrange("p t (c i) -> p c t i", i=4)
+                    at = at + step
+                    if engine == "vector":
+                        nc.vector.tensor_copy(out=dst, in_=src)
+                    else:
+                        nc.scalar.copy(out=dst, in_=src)
             return grouped
 
         def quantize_w8(name, grouped, first_tile):
@@ -98,9 +101,15 @@ def tile_list_embg_qf_res_kernel(tc, dy, w8, w4_words, w4_scales, res, wgo, offs
             )
             return acc
 
+        def new_sum(i, h, width, tag):
+            tile = keep.tile([P, width], F32, name="sum_%d_%d" % (i, h), tag=tag or "sum_%d_%d" % (i, h), align_bytes=64)
+            for c in range(0, width, HALF):
+                sums[i, h + c // HALF] = tile[:, c : c + HALF]
+            return tile
+
         def sum_on_vector(i, h):
             acc = product(i, h)
-            nc.vector.tensor_tensor(out=sums[i][:, h * HALF : (h + 1) * HALF], in0=acc[:], in1=res_of[i, h], op=ADD)
+            nc.vector.tensor_tensor(out=sums[i, h], in0=acc[:], in1=res_of[i, h], op=ADD)
 
         def sum_on_tensor(i, h):
             blocks = [slice(b * P, (b + 1) * P) for b in range(HALF // P)]
@@ -117,84 +126,77 @@ def tile_list_embg_qf_res_kernel(tc, dy, w8, w4_words, w4_scales, res, wgo, offs
             back = psum_back.tile([P, HALF], F32, name="back")
             for cols in blocks:
                 nc.tensor.transpose(back[:, cols], sum_t[:, cols], ident[:])
-            nc.scalar.copy(out=sums[i][:, h * HALF : (h + 1) * HALF], in_=back[:])
+            nc.scalar.copy(out=sums[i, h], in_=back[:])
 
-        def scatter(i, c0, c1):
+        def scatter(i, c0, c1, values):
             nc.vector.tensor_tensor(
                 out=windows[i % WINDOWS][:].indirect(offsets[:, c0 // 16 : c1 // 16]),
-                in0=sums[i][:, c0:c1], in1=weight[:, c0:c1], op=MULT,
+                in0=values, in1=weight[:, c0:c1], op=MULT,
             )
 
         def store(i):
             nc.sync.dma_start(out=out[i * P : (i + 1) * P, :], in_=windows[i % WINDOWS][:])
 
-        def late_window(tag):
-            window = keep.tile([P, T], F32, name="window%d" % len(windows), tag=tag, align_bytes=64)
-            nc.gpsimd.memset(window[:], 0.0)
-            windows.append(window)
+        def unit(route, i, h, tag=None):
+            values = new_sum(i, h, HALF, tag)
+            route(i, h)
+            scatter(i, h * HALF, (h + 1) * HALF, values[:])
 
         res_of = {}
         w8_of = {}
 
         nc.vector.memset(w4_plane[:].bitcast(I32), 0)
         make_identity(nc, ident[:])
-        for w in range(2):
+        for w in range(WINDOWS):
             nc.vector.memset(windows[w][:], 0.0)
 
-        raw_00 = load_rows("raw_00", dy[0:K_PASS, 0:HALF])
-        raw_wa = load_rows("raw_wa", w8[:, 0:256])
+        raw_00a = load_rows("raw_00a", dy[0:K_PASS, 0:256])
+        raw_00b = load_rows("raw_00b", dy[0:K_PASS, 256:HALF])
         staged = keep.tile([P, N // 4], I32, name="staged")
         for q in range(4):
             rows = slice(32 * q, 32 * q + 4)
             nc.sync.dma_start(out=staged[rows, :], in_=w4_scales[0, 4 * q : 4 * q + 4, :].bitcast(I32))
             nc.vector.tensor_copy(out=w4_plane[:].bitcast(I32)[rows, :], in_=staged[rows, :])
+        raw_wa = load_rows("raw_wa", w8[:, 0:256])
         raw_10a = load_rows("raw_10a", dy[K_PASS:K, 0:256])
         raw_10b = load_rows("raw_10b", dy[K_PASS:K, 256:HALF])
         nc.sync.dma_start(out=w4_codes[:].bitcast(I32), in_=w4_words[0].bitcast(I32))
         load_res(0, 1, 0, HALF)
         nc.sync.dma_start(offsets[:], offs)
         nc.sync.dma_start(out=weight[:, 0:HALF], in_=wgo[:, 0:HALF])
-        load_res(1, 1, 0, HALF)
         raw_wb = load_rows("raw_wb", w8[:, 256:512])
-        load_res(2, 1, 0, HALF)
+        load_res(1, 1, 0, HALF)
         raw_01 = load_rows("raw_01", dy[0:K_PASS, HALF:J])
-        raw_11 = load_rows("raw_11", dy[K_PASS:K, HALF:J])
-        load_res(3, 1, 0, HALF)
+        raw_11a = load_rows("raw_11a", dy[K_PASS:K, HALF:768])
+        raw_11b = load_rows("raw_11b", dy[K_PASS:K, 768:J])
+        raw_wc = load_rows("raw_wc", w8[:, 512:N])
+        load_res(2, 2, 0, HALF)
         load_res(0, 2, HALF, J)
         nc.sync.dma_start(out=weight[:, HALF:J], in_=wgo[:, HALF:J])
         load_res(2, 2, HALF, J)
-        raw_wc = load_rows("raw_wc", w8[:, 512:N])
         load_res(4, 2, 0, J)
         load_res(6, 2, 0, J)
 
-        quantize_dy(interleave("vector", "g_00", raw_00, 512), 0, 0, 0)
-        quantize_w8("wa", interleave("scalar", "g_wa", raw_wa, 256), 0)
-        quantize_dy(interleave("vector", "g_10a", raw_10a, 256), 1, 0, 0)
-        quantize_dy(interleave("vector", "g_10b", raw_10b, 256), 1, 0, 256)
+        quantize_dy(interleave("scalar", "g_00a", [raw_00a], 256), 0, 0, 0)
+        quantize_dy(interleave("scalar", "g_00b", [raw_00b], 256), 0, 0, 256)
+        quantize_w8("wa", interleave("scalar", "g_wa", [raw_wa], 256), 0)
+        quantize_dy(interleave("vector", "g_10a", [raw_10a], 256), 1, 0, 0)
+        quantize_dy(interleave("vector", "g_10b", [raw_10b], 256), 1, 0, 256)
 
-        late_window("g_10b")
-        sum_on_vector(0, 0)
-        late_window("res_0_0")
-        scatter(0, 0, HALF)
-        sum_on_tensor(1, 0)
-        scatter(1, 0, HALF)
-        quantize_w8("wb", interleave("scalar", "g_wb", raw_wb, 256), 2)
-        sum_on_tensor(2, 0)
-        scatter(2, 0, HALF)
-        quantize_dy(interleave("scalar", "g_01", raw_01, 256), 0, 1, 0)
-        quantize_dy(interleave("scalar", "g_11", raw_11, 256), 1, 1, 0)
-        sum_on_tensor(3, 0)
-        scatter(3, 0, HALF)
-        sum_on_vector(0, 1)
-        scatter(0, HALF, J)
-        store(0)
-        quantize_w8("wc", interleave("scalar", "g_wc", raw_wc, 256), 4)
-        for i in range(1, 4):
-            sum_on_tensor(i, 1)
-            scatter(i, HALF, J)
+        unit(sum_on_vector, 0, 0)
+        quantize_w8("wb", interleave("scalar", "g_wb", [raw_wb], 256), 2)
+        unit(sum_on_vector, 1, 0, "g_wb")
+        quantize_dy(interleave("scalar", "g_01", [raw_01], 256), 0, 1, 0)
+        quantize_dy(interleave("scalar", "g_11", [raw_11a, raw_11b], 256), 1, 1, 0)
+        unit(sum_on_vector, 2, 0, "g_11")
+        quantize_w8("wc", interleave("scalar", "g_wc", [raw_wc], 256), 4)
+        unit(sum_on_tensor, 3, 0)
+        for i in range(4):
+            unit(sum_on_tensor, i, 1)
             store(i)
         for i in range(4, TILES):
+            values = new_sum(i, 0, J, None)
             sum_on_tensor(i, 0)
             sum_on_tensor(i, 1)
-            scatter(i, 0, J)
+            scatter(i, 0, J, values[:])
             store(i)

@@ -31,9 +31,9 @@ def tile_list_embg_qf_res_kernel(tc, dy, w8, w4_words, w4_scales, res, wgo, offs
     with ExitStack() as ctx:
         keep = ctx.enter_context(tc.tile_pool(name="keep", bufs=1))
         ring = ctx.enter_context(tc.tile_pool(name="ring", bufs=3))
-        psum_mx = ctx.enter_context(tc.psum_pool(name="psum_mx", bufs=4))
-        psum_turn = ctx.enter_context(tc.psum_pool(name="psum_turn", bufs=2))
-        psum_back = ctx.enter_context(tc.psum_pool(name="psum_back", bufs=2))
+        psum_mx = ctx.enter_context(tc.psum_pool(name="psum_mx", bufs=2))
+        psum_turn = ctx.enter_context(tc.psum_pool(name="psum_turn", bufs=3))
+        psum_back = ctx.enter_context(tc.psum_pool(name="psum_back", bufs=3))
 
         offsets = keep.tile([P, J // 16], U16, name="offsets")
         weight = keep.tile([P, J], F32, name="weight")
@@ -50,7 +50,7 @@ def tile_list_embg_qf_res_kernel(tc, dy, w8, w4_words, w4_scales, res, wgo, offs
                 dy_plane[a, h] = keep.tile([P, HALF], U8, name="dy_plane%d%d" % (a, h), align_bytes=64)
 
         def load_rows(name, rows):
-            raw = keep.tile([P, PACK, rows.shape[1]], F32, name=name)
+            raw = keep.tile([P, PACK, rows.shape[1]], F32, name=name, tag=name)
             nc.sync.dma_start(out=raw[:], in_=rows.rearrange("(p t) c -> p t c", t=PACK))
             return raw
 
@@ -76,9 +76,9 @@ def tile_list_embg_qf_res_kernel(tc, dy, w8, w4_words, w4_scales, res, wgo, offs
                         nc.scalar.copy(out=dst, in_=src)
             return grouped
 
-        def quantize_w8(name, grouped, first_tile):
+        def quantize_w8(name, grouped, first_tile, tag=None):
             width = grouped.shape[1] // PACK
-            codes = keep.tile([P, width], U32, name=name + "_codes", align_bytes=64)
+            codes = keep.tile([P, width], U32, name=name + "_codes", tag=tag or name + "_codes", align_bytes=64)
             plane = keep.tile([P, width], U8, name=name + "_plane", align_bytes=64)
             nc.vector.quantize_mx(out=codes[:].bitcast(E4M3), scales=plane[:], in_=grouped[:])
             for d in range(width // P):
@@ -111,16 +111,18 @@ def tile_list_embg_qf_res_kernel(tc, dy, w8, w4_words, w4_scales, res, wgo, offs
             acc = product(i, h)
             nc.vector.tensor_tensor(out=sums[i, h], in0=acc[:], in1=res_of[i, h], op=ADD)
 
+        def product_to_sbuf(i, h, tag=None):
+            acc = product(i, h)
+            dx_of[i, h] = keep.tile([P, HALF], F32, name="dx_%d_%d" % (i, h), tag=tag or "dx_%d_%d" % (i, h))
+            nc.scalar.copy(out=dx_of[i, h][:], in_=acc[:])
+
         def sum_on_tensor(i, h):
             blocks = [slice(b * P, (b + 1) * P) for b in range(HALF // P)]
             turned = psum_turn.tile([P, HALF], F32, name="turned")
             for b, cols in enumerate(blocks):
                 nc.tensor.matmul(turned[:, cols], res_of[i, h][:, cols], ident[:], start=(b == 0), stop=False, is_transpose=True)
-            acc = product(i, h)
-            dx = ring.tile([P, HALF], F32, name="dx")
-            nc.scalar.copy(out=dx[:], in_=acc[:])
             for b, cols in enumerate(blocks):
-                nc.tensor.matmul(turned[:, cols], dx[:, cols], ident[:], start=False, stop=(b == len(blocks) - 1), is_transpose=True)
+                nc.tensor.matmul(turned[:, cols], dx_of[i, h][:, cols], ident[:], start=False, stop=(b == len(blocks) - 1), is_transpose=True)
             sum_t = ring.tile([P, HALF], F32, name="sum_t")
             nc.scalar.copy(out=sum_t[:], in_=turned[:])
             back = psum_back.tile([P, HALF], F32, name="back")
@@ -143,12 +145,13 @@ def tile_list_embg_qf_res_kernel(tc, dy, w8, w4_words, w4_scales, res, wgo, offs
             scatter(i, h * HALF, (h + 1) * HALF, values[:])
 
         res_of = {}
+        dx_of = {}
         w8_of = {}
 
         nc.vector.memset(w4_plane[:].bitcast(I32), 0)
         make_identity(nc, ident[:])
         for w in range(WINDOWS):
-            nc.vector.memset(windows[w][:], 0.0)
+            nc.vector.memset(windows[w][:].bitcast(I32), 0)
 
         raw_00a = load_rows("raw_00a", dy[0:K_PASS, 0:256])
         raw_00b = load_rows("raw_00b", dy[0:K_PASS, 256:HALF])
@@ -169,8 +172,8 @@ def tile_list_embg_qf_res_kernel(tc, dy, w8, w4_words, w4_scales, res, wgo, offs
         raw_01 = load_rows("raw_01", dy[0:K_PASS, HALF:J])
         raw_11a = load_rows("raw_11a", dy[K_PASS:K, HALF:768])
         raw_11b = load_rows("raw_11b", dy[K_PASS:K, 768:J])
-        raw_wc = load_rows("raw_wc", w8[:, 512:N])
         load_res(2, 2, 0, HALF)
+        raw_wc = load_rows("raw_wc", w8[:, 512:N])
         load_res(0, 2, HALF, J)
         nc.sync.dma_start(out=weight[:, HALF:J], in_=wgo[:, HALF:J])
         load_res(2, 2, HALF, J)
@@ -184,16 +187,26 @@ def tile_list_embg_qf_res_kernel(tc, dy, w8, w4_words, w4_scales, res, wgo, offs
         quantize_dy(interleave("vector", "g_10b", [raw_10b], 256), 1, 0, 256)
 
         unit(sum_on_vector, 0, 0)
-        quantize_w8("wb", interleave("scalar", "g_wb", [raw_wb], 256), 2)
+        quantize_w8("wb", interleave("scalar", "g_wb", [raw_wb], 256), 2, "sum_0_0")
         unit(sum_on_vector, 1, 0, "g_wb")
         quantize_dy(interleave("scalar", "g_01", [raw_01], 256), 0, 1, 0)
         quantize_dy(interleave("scalar", "g_11", [raw_11a, raw_11b], 256), 1, 1, 0)
         unit(sum_on_vector, 2, 0, "g_11")
         quantize_w8("wc", interleave("scalar", "g_wc", [raw_wc], 256), 4)
+        product_to_sbuf(3, 0, "raw_11b")
         unit(sum_on_tensor, 3, 0)
-        for i in range(4):
+        for i in range(2):
+            product_to_sbuf(i, 1)
             unit(sum_on_tensor, i, 1)
             store(i)
+        for i, h in ((2, 1), (3, 1), (4, 0), (4, 1)):
+            product_to_sbuf(i, h)
+        for i in range(2, 4):
+            unit(sum_on_tensor, i, 1)
+            store(i)
+        for i in range(5, TILES):
+            product_to_sbuf(i, 0)
+            product_to_sbuf(i, 1)
         for i in range(4, TILES):
             values = new_sum(i, 0, J, None)
             sum_on_tensor(i, 0)

@@ -153,16 +153,14 @@ def tile_list_embg_qf_res_kernel(tc, dy, w8, w4_words, w4_scales, res, wgo, offs
         for w in range(WINDOWS):
             nc.vector.memset(windows[w][:].bitcast(I32), 0)
 
-        raw_00a = load_rows("raw_00a", dy[0:K_PASS, 0:256])
-        raw_00b = load_rows("raw_00b", dy[0:K_PASS, 256:HALF])
+        raw_00 = load_rows("raw_00", dy[0:K_PASS, 0:HALF])
         staged = keep.tile([P, N // 4], I32, name="staged")
         for q in range(4):
             rows = slice(32 * q, 32 * q + 4)
             nc.sync.dma_start(out=staged[rows, :], in_=w4_scales[0, 4 * q : 4 * q + 4, :].bitcast(I32))
             nc.vector.tensor_copy(out=w4_plane[:].bitcast(I32)[rows, :], in_=staged[rows, :])
         raw_wa = load_rows("raw_wa", w8[:, 0:256])
-        raw_10a = load_rows("raw_10a", dy[K_PASS:K, 0:256])
-        raw_10b = load_rows("raw_10b", dy[K_PASS:K, 256:HALF])
+        raw_10 = load_rows("raw_10", dy[K_PASS:K, 0:HALF])
         nc.sync.dma_start(out=w4_codes[:].bitcast(I32), in_=w4_words[0].bitcast(I32))
         load_res(0, 1, 0, HALF)
         nc.sync.dma_start(offsets[:], offs)
@@ -180,11 +178,11 @@ def tile_list_embg_qf_res_kernel(tc, dy, w8, w4_words, w4_scales, res, wgo, offs
         load_res(4, 2, 0, J)
         load_res(6, 2, 0, J)
 
-        quantize_dy(interleave("scalar", "g_00a", [raw_00a], 256), 0, 0, 0)
-        quantize_dy(interleave("scalar", "g_00b", [raw_00b], 256), 0, 0, 256)
+        quantize_dy(interleave("scalar", "g_00a", [raw_00[:, :, 0:256]], 256), 0, 0, 0)
+        quantize_dy(interleave("scalar", "g_00b", [raw_00[:, :, 256:HALF]], 256), 0, 0, 256)
         quantize_w8("wa", interleave("scalar", "g_wa", [raw_wa], 256), 0)
-        quantize_dy(interleave("vector", "g_10a", [raw_10a], 256), 1, 0, 0)
-        quantize_dy(interleave("vector", "g_10b", [raw_10b], 256), 1, 0, 256)
+        quantize_dy(interleave("vector", "g_10a", [raw_10[:, :, 0:256]], 256), 1, 0, 0)
+        quantize_dy(interleave("scalar", "g_10b", [raw_10[:, :, 256:HALF]], 256), 1, 0, 256)
 
         unit(sum_on_vector, 0, 0)
         quantize_w8("wb", interleave("scalar", "g_wb", [raw_wb], 256), 2, "sum_0_0")

@@ -30,10 +30,7 @@ def tile_list_embg_qf_res_kernel(tc, dy, w8, w4_words, w4_scales, res, wgo, offs
     nc = tc.nc
     with ExitStack() as ctx:
         keep = ctx.enter_context(tc.tile_pool(name="keep", bufs=1))
-        ring = ctx.enter_context(tc.tile_pool(name="ring", bufs=3))
-        psum_mx = ctx.enter_context(tc.psum_pool(name="psum_mx", bufs=2))
-        psum_turn = ctx.enter_context(tc.psum_pool(name="psum_turn", bufs=3))
-        psum_back = ctx.enter_context(tc.psum_pool(name="psum_back", bufs=3))
+        psum = ctx.enter_context(tc.psum_pool(name="psum", bufs=1))
 
         offsets = keep.tile([P, J // 16], U16, name="offsets")
         weight = keep.tile([P, J], F32, name="weight")
@@ -61,9 +58,13 @@ def tile_list_embg_qf_res_kernel(tc, dy, w8, w4_words, w4_scales, res, wgo, offs
                 for c in range(c0, c1, HALF):
                     res_of[i + d, c // HALF] = raw[:, d, c - c0 : c - c0 + HALF]
 
-        def interleave(engine, name, raws, step):
+        def load_w4(i, count):
+            cols = slice(2 * P * i, 2 * P * (i + count))
+            nc.sync.dma_start(out=w4_codes[:, cols].bitcast(I32), in_=w4_words[0][:, cols].bitcast(I32))
+
+        def interleave(engine, name, raws, step, tag=None):
             width = sum(raw.shape[2] for raw in raws)
-            grouped = keep.tile([P, width * PACK], BF16, name=name, tag=name, align_bytes=64)
+            grouped = keep.tile([P, width * PACK], BF16, name=name, tag=tag or name, align_bytes=64)
             at = 0
             for raw in raws:
                 for c in range(0, raw.shape[2], step):
@@ -88,17 +89,28 @@ def tile_list_embg_qf_res_kernel(tc, dy, w8, w4_words, w4_scales, res, wgo, offs
             cols = slice(c0, c0 + grouped.shape[1] // PACK)
             nc.vector.quantize_mx(out=dy_codes[a, h][:, cols].bitcast(E5M2), scales=dy_plane[a, h][:, cols], in_=grouped[:])
 
+        def product_bank(i, h):
+            if i >= 4:
+                return "acc%d" % h
+            if h == 0:
+                return "acc%d" % (i % 2)
+            return "acc%d" % (i % 2)
+
         def product(i, h):
-            acc = psum_mx.tile([P, HALF], F32, name="acc")
+            acc = psum.tile([P, HALF], F32, name="acc", tag=product_bank(i, h))
             codes, plane = w8_of[i]
             nc.tensor.matmul_mx(
                 out=acc[:], lhsT=codes.bitcast(E4M3), lhsT_scale=plane,
                 rhs=dy_codes[0, h][:].bitcast(E5M2), rhs_scale=dy_plane[0, h][:], start=True, stop=False,
             )
-            nc.tensor.matmul_mx(
-                out=acc[:], lhsT=w4_codes[:, 2 * P * i : 2 * P * (i + 1)].bitcast(E2M1), lhsT_scale=w4_plane[:, P * i : P * (i + 1)],
-                rhs=dy_codes[1, h][:].bitcast(E5M2), rhs_scale=dy_plane[1, h][:], start=False, stop=True,
-            )
+            step = HALF // 2 if (i, h) == (0, 0) else HALF
+            for c in range(0, HALF, step):
+                nc.tensor.matmul_mx(
+                    out=acc[:, c : c + step],
+                    lhsT=w4_codes[:, 2 * P * i : 2 * P * (i + 1)].bitcast(E2M1), lhsT_scale=w4_plane[:, P * i : P * (i + 1)],
+                    rhs=dy_codes[1, h][:, c : c + step].bitcast(E5M2), rhs_scale=dy_plane[1, h][:, c : c + step],
+                    start=False, stop=(c + step == HALF),
+                )
             return acc
 
         def new_sum(i, h, width, tag):
@@ -118,14 +130,14 @@ def tile_list_embg_qf_res_kernel(tc, dy, w8, w4_words, w4_scales, res, wgo, offs
 
         def sum_on_tensor(i, h):
             blocks = [slice(b * P, (b + 1) * P) for b in range(HALF // P)]
-            turned = psum_turn.tile([P, HALF], F32, name="turned")
+            turned = psum.tile([P, HALF], F32, name="turned", tag="turn%d" % ((2 * i + h) % 3))
             for b, cols in enumerate(blocks):
                 nc.tensor.matmul(turned[:, cols], res_of[i, h][:, cols], ident[:], start=(b == 0), stop=False, is_transpose=True)
             for b, cols in enumerate(blocks):
                 nc.tensor.matmul(turned[:, cols], dx_of[i, h][:, cols], ident[:], start=False, stop=(b == len(blocks) - 1), is_transpose=True)
-            sum_t = ring.tile([P, HALF], F32, name="sum_t")
+            sum_t = keep.tile([P, HALF], F32, name="sum_t", tag="sum_t%d%d" % ((i, h) if i < 4 else (4 + i % 2, h)), align_bytes=64)
             nc.scalar.copy(out=sum_t[:], in_=turned[:])
-            back = psum_back.tile([P, HALF], F32, name="back")
+            back = psum.tile([P, HALF], F32, name="back", tag="back%d" % ((2 * i + h) % 3))
             for cols in blocks:
                 nc.tensor.transpose(back[:, cols], sum_t[:, cols], ident[:])
             nc.scalar.copy(out=sums[i, h], in_=back[:])
@@ -159,55 +171,83 @@ def tile_list_embg_qf_res_kernel(tc, dy, w8, w4_words, w4_scales, res, wgo, offs
             rows = slice(32 * q, 32 * q + 4)
             nc.sync.dma_start(out=staged[rows, :], in_=w4_scales[0, 4 * q : 4 * q + 4, :].bitcast(I32))
             nc.vector.tensor_copy(out=w4_plane[:].bitcast(I32)[rows, :], in_=staged[rows, :])
-        raw_wa = load_rows("raw_wa", w8[:, 0:256])
-        raw_10 = load_rows("raw_10", dy[K_PASS:K, 0:HALF])
-        nc.sync.dma_start(out=w4_codes[:].bitcast(I32), in_=w4_words[0].bitcast(I32))
+        raw_w0 = load_rows("raw_w0", w8[:, 0:P])
+        raw_10a = load_rows("raw_10a", dy[K_PASS:K, 0:256])
+        raw_10b = load_rows("raw_10b", dy[K_PASS:K, 256:HALF])
+        raw_w1 = load_rows("raw_w1", w8[:, P:256])
+        load_w4(0, 2)
         load_res(0, 1, 0, HALF)
         nc.sync.dma_start(offsets[:], offs)
         nc.sync.dma_start(out=weight[:, 0:HALF], in_=wgo[:, 0:HALF])
         raw_wb = load_rows("raw_wb", w8[:, 256:512])
+        load_w4(2, 2)
         load_res(1, 1, 0, HALF)
+        load_res(2, 2, 0, HALF)
         raw_01 = load_rows("raw_01", dy[0:K_PASS, HALF:J])
         raw_11a = load_rows("raw_11a", dy[K_PASS:K, HALF:768])
         raw_11b = load_rows("raw_11b", dy[K_PASS:K, 768:J])
-        load_res(2, 2, 0, HALF)
-        raw_wc = load_rows("raw_wc", w8[:, 512:N])
+        raw_wc = load_rows("raw_wc", w8[:, 512:768])
         load_res(0, 2, HALF, J)
         nc.sync.dma_start(out=weight[:, HALF:J], in_=wgo[:, HALF:J])
         load_res(2, 2, HALF, J)
+        raw_wd = load_rows("raw_wd", w8[:, 768:N])
+        load_w4(4, 4)
         load_res(4, 2, 0, J)
         load_res(6, 2, 0, J)
 
+        def shared(name, raw):
+            grouped = keep.tile([P, 256 * PACK], BF16, name=name, tag=name, align_bytes=64)
+            for engine, c0, c1 in ((nc.scalar.copy, 160, 256), (nc.vector.tensor_copy, 0, 160)):
+                engine(
+                    out=grouped[:, c0 * PACK : c1 * PACK].rearrange("p (c i t) -> p c t i", i=4, t=PACK),
+                    in_=raw[:, :, c0:c1].rearrange("p t (c i) -> p c t i", i=4),
+                )
+            return grouped
+
         quantize_dy(interleave("scalar", "g_00a", [raw_00[:, :, 0:256]], 256), 0, 0, 0)
-        quantize_dy(interleave("scalar", "g_00b", [raw_00[:, :, 256:HALF]], 256), 0, 0, 256)
-        quantize_w8("wa", interleave("scalar", "g_wa", [raw_wa], 256), 0)
-        quantize_dy(interleave("vector", "g_10a", [raw_10[:, :, 0:256]], 256), 1, 0, 0)
-        quantize_dy(interleave("scalar", "g_10b", [raw_10[:, :, 256:HALF]], 256), 1, 0, 256)
+        quantize_dy(interleave("vector", "g_00b", [raw_00[:, :, 256:HALF]], 256), 0, 0, 256)
+        quantize_w8("w0", interleave("scalar", "g_w0", [raw_w0], P), 0)
+        quantize_dy(interleave("scalar", "g_10a", [raw_10a], 256), 1, 0, 0)
+        quantize_dy(shared("g_10b", raw_10b), 1, 0, 256)
+        quantize_w8("w1", interleave("scalar", "g_w1", [raw_w1], P), 1)
+
+        def summed(route, i, h):
+            new_sum(i, h, HALF, None)
+            route(i, h)
+
+        def place(i, h):
+            scatter(i, h * HALF, (h + 1) * HALF, sums[i, h])
 
         unit(sum_on_vector, 0, 0)
-        quantize_w8("wb", interleave("scalar", "g_wb", [raw_wb], 256), 2, "sum_0_0")
-        unit(sum_on_vector, 1, 0, "g_wb")
+        summed(sum_on_vector, 1, 0)
+        quantize_w8("wb", interleave("scalar", "g_wb", [raw_wb], 256), 2)
+        place(1, 0)
+        unit(sum_on_vector, 2, 0)
+        product_to_sbuf(3, 0)
         quantize_dy(interleave("scalar", "g_01", [raw_01], 256), 0, 1, 0)
-        quantize_dy(interleave("scalar", "g_11", [raw_11a, raw_11b], 256), 1, 1, 0)
-        unit(sum_on_vector, 2, 0, "g_11")
-        quantize_w8("wc", interleave("scalar", "g_wc", [raw_wc], 256), 4)
-        product_to_sbuf(3, 0, "raw_11b")
         unit(sum_on_tensor, 3, 0)
+        quantize_dy(interleave("scalar", "g_11", [raw_11a, raw_11b], 256), 1, 1, 0)
+        quantize_w8("wc", interleave("scalar", "g_wc", [raw_wc], 256), 4, "g_11")
+        summed(sum_on_vector, 0, 1)
+        summed(sum_on_vector, 1, 1)
         for i in range(2):
-            product_to_sbuf(i, 1)
-            unit(sum_on_tensor, i, 1)
+            place(i, 1)
             store(i)
-        for i, h in ((2, 1), (3, 1), (4, 0), (4, 1)):
-            product_to_sbuf(i, h)
-        for i in range(2, 4):
-            unit(sum_on_tensor, i, 1)
-            store(i)
-        for i in range(5, TILES):
-            product_to_sbuf(i, 0)
-            product_to_sbuf(i, 1)
+        product_to_sbuf(2, 1)
+        product_to_sbuf(3, 1)
+        grouped_wd = interleave("scalar", "g_wd", [raw_wd], 256)
+        summed(sum_on_tensor, 2, 1)
+        place(2, 1)
+        store(2)
+        summed(sum_on_tensor, 3, 1)
+        quantize_w8("wd", grouped_wd, 6, "sum_t31")
+        place(3, 1)
+        store(3)
         for i in range(4, TILES):
             values = new_sum(i, 0, J, None)
-            sum_on_tensor(i, 0)
-            sum_on_tensor(i, 1)
+            for h in range(2):
+                product_to_sbuf(i, h)
+            for h in range(2):
+                sum_on_tensor(i, h)
             scatter(i, 0, J, values[:])
             store(i)

@@ -23,7 +23,6 @@ PACK = 4
 K_PASS = P * PACK
 HALF = 512
 TILES = N // P
-WINDOWS = 4
 
 
 def tile_list_embg_qf_res_kernel(tc, dy, w8, w4_words, w4_scales, res, wgo, offs, out):
@@ -37,22 +36,30 @@ def tile_list_embg_qf_res_kernel(tc, dy, w8, w4_words, w4_scales, res, wgo, offs
         w4_codes = keep.tile([P, 2 * N], U8, name="w4_codes", align_bytes=64)
         w4_plane = keep.tile([P, N], U8, name="w4_plane", align_bytes=64)
         ident = keep.tile([P, P], F32, name="ident")
-        windows = [keep.tile([P, T], F32, name="window%d" % w) for w in range(WINDOWS)]
+        windows = {}
         sums = {}
         dy_codes = {}
         dy_plane = {}
         for a in range(2):
-            for h in range(2):
-                dy_codes[a, h] = keep.tile([P, HALF], U32, name="dy_codes%d%d" % (a, h), align_bytes=64)
-                dy_plane[a, h] = keep.tile([P, HALF], U8, name="dy_plane%d%d" % (a, h), align_bytes=64)
+            dy_codes[a, 0] = keep.tile([P, HALF], U32, name="dy_codes%d" % a, align_bytes=64)[:]
+            dy_plane[a, 0] = keep.tile([P, HALF], U8, name="dy_plane%d" % a, align_bytes=64)[:]
+        late_codes = keep.tile([P, 2 * HALF], U32, name="late_codes", align_bytes=64)
+        late_plane = keep.tile([P, 2 * HALF], U8, name="late_plane", align_bytes=64)
+        for a in range(2):
+            dy_codes[a, 1] = late_codes[:, a * HALF : (a + 1) * HALF]
+            dy_plane[a, 1] = late_plane[:, a * HALF : (a + 1) * HALF]
+
+        def clear_window(engine, i):
+            windows[i] = keep.tile([P, T], F32, name="window%d" % i, tag="window%d" % i, align_bytes=64)
+            engine.memset(windows[i][:].bitcast(I32), 0)
 
         def load_rows(name, rows):
-            raw = keep.tile([P, PACK, rows.shape[1]], F32, name=name, tag=name)
+            raw = keep.tile([P, PACK, rows.shape[1]], F32, name=name, tag=name, align_bytes=64)
             nc.sync.dma_start(out=raw[:], in_=rows.rearrange("(p t) c -> p t c", t=PACK))
             return raw
 
-        def load_res(i, count, c0, c1):
-            raw = keep.tile([P, count, c1 - c0], F32, name="res_%d_%d" % (i, c0), tag="res_%d_%d" % (i, c0), align_bytes=64)
+        def load_res(i, count, c0, c1, tag=None):
+            raw = keep.tile([P, count, c1 - c0], F32, name="res_%d_%d" % (i, c0), tag=tag or "res_%d_%d" % (i, c0), align_bytes=64)
             nc.sync.dma_start(out=raw[:], in_=res[i * P : (i + count) * P, c0:c1].rearrange("(i p) c -> p i c", p=P))
             for d in range(count):
                 for c in range(c0, c1, HALF):
@@ -89,19 +96,12 @@ def tile_list_embg_qf_res_kernel(tc, dy, w8, w4_words, w4_scales, res, wgo, offs
             cols = slice(c0, c0 + grouped.shape[1] // PACK)
             nc.vector.quantize_mx(out=dy_codes[a, h][:, cols].bitcast(E5M2), scales=dy_plane[a, h][:, cols], in_=grouped[:])
 
-        def product_bank(i, h):
-            if i >= 4:
-                return "acc%d" % h
-            if h == 0:
-                return "acc%d" % (i % 2)
-            return "acc%d" % (i % 2)
-
-        def product(i, h):
-            acc = psum.tile([P, HALF], F32, name="acc", tag=product_bank(i, h))
+        def product(i, h, bank):
+            acc = psum.tile([P, HALF], F32, name="acc", tag=bank)
             codes, plane = w8_of[i]
             nc.tensor.matmul_mx(
                 out=acc[:], lhsT=codes.bitcast(E4M3), lhsT_scale=plane,
-                rhs=dy_codes[0, h][:].bitcast(E5M2), rhs_scale=dy_plane[0, h][:], start=True, stop=False,
+                rhs=dy_codes[0, h].bitcast(E5M2), rhs_scale=dy_plane[0, h], start=True, stop=False,
             )
             step = HALF // 2 if (i, h) == (0, 0) else HALF
             for c in range(0, HALF, step):
@@ -113,48 +113,41 @@ def tile_list_embg_qf_res_kernel(tc, dy, w8, w4_words, w4_scales, res, wgo, offs
                 )
             return acc
 
-        def new_sum(i, h, width, tag):
-            tile = keep.tile([P, width], F32, name="sum_%d_%d" % (i, h), tag=tag or "sum_%d_%d" % (i, h), align_bytes=64)
-            for c in range(0, width, HALF):
-                sums[i, h + c // HALF] = tile[:, c : c + HALF]
-            return tile
+        def sum_on_vector(i, bank):
+            acc = product(i, 0, bank)
+            sums[i, 0] = keep.tile([P, HALF], F32, name="sum_%d" % i, align_bytes=64)[:]
+            nc.vector.tensor_tensor(out=sums[i, 0], in0=acc[:], in1=res_of[i, 0], op=ADD)
 
-        def sum_on_vector(i, h):
-            acc = product(i, h)
-            nc.vector.tensor_tensor(out=sums[i, h], in0=acc[:], in1=res_of[i, h], op=ADD)
-
-        def product_to_sbuf(i, h, tag=None):
-            acc = product(i, h)
-            dx_of[i, h] = keep.tile([P, HALF], F32, name="dx_%d_%d" % (i, h), tag=tag or "dx_%d_%d" % (i, h))
+        def product_to_sbuf(i, h, bank):
+            acc = product(i, h, bank)
+            dx_of[i, h] = keep.tile([P, HALF], F32, name="dx_%d_%d" % (i, h), align_bytes=64)
             nc.scalar.copy(out=dx_of[i, h][:], in_=acc[:])
 
-        def sum_on_tensor(i, h):
-            blocks = [slice(b * P, (b + 1) * P) for b in range(HALF // P)]
-            turned = psum.tile([P, HALF], F32, name="turned", tag="turn%d" % ((2 * i + h) % 3))
+        blocks = [slice(b * P, (b + 1) * P) for b in range(HALF // P)]
+
+        def turn_and_add(i, h, bank):
+            turned = psum.tile([P, HALF], F32, name="turned", tag=bank)
             for b, cols in enumerate(blocks):
                 nc.tensor.matmul(turned[:, cols], res_of[i, h][:, cols], ident[:], start=(b == 0), stop=False, is_transpose=True)
             for b, cols in enumerate(blocks):
                 nc.tensor.matmul(turned[:, cols], dx_of[i, h][:, cols], ident[:], start=False, stop=(b == len(blocks) - 1), is_transpose=True)
-            sum_t = keep.tile([P, HALF], F32, name="sum_t", tag="sum_t%d%d" % ((i, h) if i < 4 else (4 + i % 2, h)), align_bytes=64)
-            nc.scalar.copy(out=sum_t[:], in_=turned[:])
-            back = psum.tile([P, HALF], F32, name="back", tag="back%d" % ((2 * i + h) % 3))
+            nc.scalar.copy(out=dx_of[i, h][:], in_=turned[:])
+
+        def turn_back(i, h, bank, tag=None):
+            back = psum.tile([P, HALF], F32, name="back", tag=bank)
             for cols in blocks:
-                nc.tensor.transpose(back[:, cols], sum_t[:, cols], ident[:])
+                nc.tensor.transpose(back[:, cols], dx_of[i, h][:, cols], ident[:])
+            sums[i, h] = keep.tile([P, HALF], F32, name="sum_%d_%d" % (i, h), tag=tag, align_bytes=64)[:] if tag else res_of[i, h]
             nc.scalar.copy(out=sums[i, h], in_=back[:])
 
-        def scatter(i, c0, c1, values):
+        def place(i, h):
             nc.vector.tensor_tensor(
-                out=windows[i % WINDOWS][:].indirect(offsets[:, c0 // 16 : c1 // 16]),
-                in0=values, in1=weight[:, c0:c1], op=MULT,
+                out=windows[i][:].indirect(offsets[:, h * HALF // 16 : (h + 1) * HALF // 16]),
+                in0=sums[i, h], in1=weight[:, h * HALF : (h + 1) * HALF], op=MULT,
             )
 
         def store(i):
-            nc.sync.dma_start(out=out[i * P : (i + 1) * P, :], in_=windows[i % WINDOWS][:])
-
-        def unit(route, i, h, tag=None):
-            values = new_sum(i, h, HALF, tag)
-            route(i, h)
-            scatter(i, h * HALF, (h + 1) * HALF, values[:])
+            nc.sync.dma_start(out=out[i * P : (i + 1) * P, :], in_=windows[i][:])
 
         res_of = {}
         dx_of = {}
@@ -162,8 +155,9 @@ def tile_list_embg_qf_res_kernel(tc, dy, w8, w4_words, w4_scales, res, wgo, offs
 
         nc.vector.memset(w4_plane[:].bitcast(I32), 0)
         make_identity(nc, ident[:])
-        for w in range(WINDOWS):
-            nc.vector.memset(windows[w][:].bitcast(I32), 0)
+        clear_window(nc.vector, 0)
+        clear_window(nc.vector, 1)
+        clear_window(nc.gpsimd, 2)
 
         raw_00 = load_rows("raw_00", dy[0:K_PASS, 0:HALF])
         staged = keep.tile([P, N // 4], I32, name="staged")
@@ -176,24 +170,25 @@ def tile_list_embg_qf_res_kernel(tc, dy, w8, w4_words, w4_scales, res, wgo, offs
         raw_10b = load_rows("raw_10b", dy[K_PASS:K, 256:HALF])
         raw_w1 = load_rows("raw_w1", w8[:, P:256])
         load_w4(0, 2)
-        load_res(0, 1, 0, HALF)
+        load_res(0, 1, 0, HALF, "window3")
         nc.sync.dma_start(offsets[:], offs)
         nc.sync.dma_start(out=weight[:, 0:HALF], in_=wgo[:, 0:HALF])
-        raw_wb = load_rows("raw_wb", w8[:, 256:512])
+        raw_w23 = load_rows("raw_w23", w8[:, 256:512])
         load_w4(2, 2)
         load_res(1, 1, 0, HALF)
-        load_res(2, 2, 0, HALF)
-        raw_01 = load_rows("raw_01", dy[0:K_PASS, HALF:J])
-        raw_11a = load_rows("raw_11a", dy[K_PASS:K, HALF:768])
-        raw_11b = load_rows("raw_11b", dy[K_PASS:K, 768:J])
-        raw_wc = load_rows("raw_wc", w8[:, 512:768])
-        load_res(0, 2, HALF, J)
-        nc.sync.dma_start(out=weight[:, HALF:J], in_=wgo[:, HALF:J])
-        load_res(2, 2, HALF, J)
-        raw_wd = load_rows("raw_wd", w8[:, 768:N])
+        load_res(3, 1, 0, HALF)
+        raw_w45 = load_rows("raw_w45", w8[:, 512:768])
         load_w4(4, 4)
-        load_res(4, 2, 0, J)
-        load_res(6, 2, 0, J)
+        load_res(2, 1, 0, HALF)
+        load_res(4, 1, 0, HALF)
+        load_res(5, 1, 0, HALF)
+        raw_w67 = load_rows("raw_w67", w8[:, 768:N])
+        raw_01 = load_rows("raw_01", dy[0:K_PASS, HALF:J])
+        raw_11 = load_rows("raw_11", dy[K_PASS:K, HALF:J])
+        load_res(6, 2, 0, HALF)
+        nc.sync.dma_start(out=weight[:, HALF:J], in_=wgo[:, HALF:J])
+        for i in range(0, TILES, 2):
+            load_res(i, 2, HALF, J)
 
         def shared(name, raw):
             grouped = keep.tile([P, 256 * PACK], BF16, name=name, tag=name, align_bytes=64)
@@ -211,43 +206,62 @@ def tile_list_embg_qf_res_kernel(tc, dy, w8, w4_words, w4_scales, res, wgo, offs
         quantize_dy(shared("g_10b", raw_10b), 1, 0, 256)
         quantize_w8("w1", interleave("scalar", "g_w1", [raw_w1], P), 1)
 
-        def summed(route, i, h):
-            new_sum(i, h, HALF, None)
-            route(i, h)
+        added = [(i, 0) for i in range(3, TILES)] + [(i, 1) for i in range(TILES)]
+        turn_bank = ["turn%d" % (n % 3) for n in range(len(added))]
+        back_bank = ["back%d" % (n % 3) for n in range(len(added))]
+        product_bank = ["first0", "first0"] + turn_bank[: len(added) - 2]
+        product_bank[5] = turn_bank[4]
+        product_bank[6] = back_bank[4]
 
-        def place(i, h):
-            scatter(i, h * HALF, (h + 1) * HALF, sums[i, h])
+        def multiply(n):
+            product_to_sbuf(*added[n], product_bank[n])
 
-        unit(sum_on_vector, 0, 0)
-        summed(sum_on_vector, 1, 0)
-        quantize_w8("wb", interleave("scalar", "g_wb", [raw_wb], 256), 2)
+        def turn(n):
+            turn_and_add(*added[n], turn_bank[n])
+
+        def back(n, tag=None):
+            turn_back(*added[n], back_bank[n], tag)
+
+        sum_on_vector(0, "first0")
+        place(0, 0)
+        clear_window(nc.gpsimd, 3)
+        sum_on_vector(1, "first1")
+        quantize_w8("w23", interleave("scalar", "g_w23", [raw_w23], 256, "window4"), 2)
         place(1, 0)
-        unit(sum_on_vector, 2, 0)
-        product_to_sbuf(3, 0)
-        quantize_dy(interleave("scalar", "g_01", [raw_01], 256), 0, 1, 0)
-        unit(sum_on_tensor, 3, 0)
-        quantize_dy(interleave("scalar", "g_11", [raw_11a, raw_11b], 256), 1, 1, 0)
-        quantize_w8("wc", interleave("scalar", "g_wc", [raw_wc], 256), 4, "g_11")
-        summed(sum_on_vector, 0, 1)
-        summed(sum_on_vector, 1, 1)
-        for i in range(2):
-            place(i, 1)
-            store(i)
-        product_to_sbuf(2, 1)
-        product_to_sbuf(3, 1)
-        grouped_wd = interleave("scalar", "g_wd", [raw_wd], 256)
-        summed(sum_on_tensor, 2, 1)
-        place(2, 1)
-        store(2)
-        summed(sum_on_tensor, 3, 1)
-        quantize_w8("wd", grouped_wd, 6, "sum_t31")
-        place(3, 1)
-        store(3)
-        for i in range(4, TILES):
-            values = new_sum(i, 0, J, None)
-            for h in range(2):
-                product_to_sbuf(i, h)
-            for h in range(2):
-                sum_on_tensor(i, h)
-            scatter(i, 0, J, values[:])
-            store(i)
+        clear_window(nc.gpsimd, 4)
+        multiply(0)
+        sum_on_vector(2, "first1")
+        turn(0)
+        quantize_w8("w45", interleave("scalar", "g_w45", [raw_w45], 256, "window5"), 4)
+        place(2, 0)
+        clear_window(nc.gpsimd, 5)
+        back(0)
+        place(3, 0)
+        multiply(1)
+        multiply(2)
+        turn(1)
+        quantize_w8("w67", interleave("scalar", "g_w67", [raw_w67], 256, "window6"), 6)
+        clear_window(nc.gpsimd, 6)
+        back(1, "raw_w67")
+        place(4, 0)
+        turn(2)
+        back(2)
+        place(5, 0)
+        multiply(3)
+        multiply(4)
+        late = interleave("scalar", "g_late", [raw_01, raw_11], 256, "window7")
+        nc.vector.quantize_mx(out=late_codes[:].bitcast(E5M2), scales=late_plane[:], in_=late[:])
+        clear_window(nc.gpsimd, 7)
+        for n in (3, 4):
+            turn(n)
+            back(n)
+            place(*added[n])
+        multiply(5)
+        multiply(6)
+        for n in range(5, len(added)):
+            turn(n)
+            back(n)
+            if n + 2 < len(added):
+                multiply(n + 2)
+            place(*added[n])
+            store(added[n][0])

@@ -133,11 +133,11 @@ def tile_list_embg_qf_res_kernel(tc, dy, w8, w4_words, w4_scales, res, wgo, offs
                 nc.tensor.matmul(turned[:, cols], dx_of[i, h][:, cols], ident[:], start=False, stop=(b == len(blocks) - 1), is_transpose=True)
             nc.scalar.copy(out=dx_of[i, h][:], in_=turned[:])
 
-        def turn_back(i, h, bank, tag=None):
+        def turn_back(i, h, bank):
             back = psum.tile([P, HALF], F32, name="back", tag=bank)
             for cols in blocks:
                 nc.tensor.transpose(back[:, cols], dx_of[i, h][:, cols], ident[:])
-            sums[i, h] = keep.tile([P, HALF], F32, name="sum_%d_%d" % (i, h), tag=tag, align_bytes=64)[:] if tag else res_of[i, h]
+            sums[i, h] = res_of[i, h]
             nc.scalar.copy(out=sums[i, h], in_=back[:])
 
         def place(i, h):
@@ -180,9 +180,8 @@ def tile_list_embg_qf_res_kernel(tc, dy, w8, w4_words, w4_scales, res, wgo, offs
         raw_w45 = load_rows("raw_w45", w8[:, 512:768])
         load_w4(4, 4)
         load_res(2, 1, 0, HALF)
-        load_res(4, 1, 0, HALF)
-        load_res(5, 1, 0, HALF)
         raw_w67 = load_rows("raw_w67", w8[:, 768:N])
+        load_res(4, 2, 0, HALF)
         raw_01 = load_rows("raw_01", dy[0:K_PASS, HALF:J])
         raw_11 = load_rows("raw_11", dy[K_PASS:K, HALF:J])
         load_res(6, 2, 0, HALF)
@@ -207,11 +206,9 @@ def tile_list_embg_qf_res_kernel(tc, dy, w8, w4_words, w4_scales, res, wgo, offs
         quantize_w8("w1", interleave("scalar", "g_w1", [raw_w1], P), 1)
 
         added = [(i, 0) for i in range(3, TILES)] + [(i, 1) for i in range(TILES)]
-        turn_bank = ["turn%d" % (n % 3) for n in range(len(added))]
-        back_bank = ["back%d" % (n % 3) for n in range(len(added))]
-        product_bank = ["first0", "first0"] + turn_bank[: len(added) - 2]
-        product_bank[5] = turn_bank[4]
-        product_bank[6] = back_bank[4]
+        turn_bank = ["bank%d" % b for b in (2, 4, 6, 0, 2)] + ["bank%d" % (4, 6, 0)[i % 3] for i in range(TILES)]
+        back_bank = ["bank%d" % b for b in (3, 5, 7, 1, 3)] + ["bank%d" % (5, 7, 1)[i % 3] for i in range(TILES)]
+        product_bank = ["bank%d" % b for b in (0, 2, 3, 6, 7)] + ["bank%d" % (2 + i % 2) for i in range(TILES)]
 
         def multiply(n):
             product_to_sbuf(*added[n], product_bank[n])
@@ -219,34 +216,32 @@ def tile_list_embg_qf_res_kernel(tc, dy, w8, w4_words, w4_scales, res, wgo, offs
         def turn(n):
             turn_and_add(*added[n], turn_bank[n])
 
-        def back(n, tag=None):
-            turn_back(*added[n], back_bank[n], tag)
+        def back(n):
+            turn_back(*added[n], back_bank[n])
 
-        sum_on_vector(0, "first0")
+        sum_on_vector(0, "bank0")
         place(0, 0)
         clear_window(nc.gpsimd, 3)
-        sum_on_vector(1, "first1")
+        sum_on_vector(1, "bank1")
         quantize_w8("w23", interleave("scalar", "g_w23", [raw_w23], 256, "window4"), 2)
         place(1, 0)
         clear_window(nc.gpsimd, 4)
         multiply(0)
-        sum_on_vector(2, "first1")
+        sum_on_vector(2, "bank1")
         turn(0)
         quantize_w8("w45", interleave("scalar", "g_w45", [raw_w45], 256, "window5"), 4)
         place(2, 0)
         clear_window(nc.gpsimd, 5)
         back(0)
+        quantize_w8("w67", interleave("scalar", "g_w67", [raw_w67], 256, "window6"), 6)
         place(3, 0)
+        clear_window(nc.gpsimd, 6)
         multiply(1)
         multiply(2)
-        turn(1)
-        quantize_w8("w67", interleave("scalar", "g_w67", [raw_w67], 256, "window6"), 6)
-        clear_window(nc.gpsimd, 6)
-        back(1, "raw_w67")
-        place(4, 0)
-        turn(2)
-        back(2)
-        place(5, 0)
+        for n in (1, 2):
+            turn(n)
+            back(n)
+            place(*added[n])
         multiply(3)
         multiply(4)
         late = interleave("scalar", "g_late", [raw_01, raw_11], 256, "window7")
@@ -260,8 +255,8 @@ def tile_list_embg_qf_res_kernel(tc, dy, w8, w4_words, w4_scales, res, wgo, offs
         multiply(6)
         for n in range(5, len(added)):
             turn(n)
-            back(n)
             if n + 2 < len(added):
                 multiply(n + 2)
+            back(n)
             place(*added[n])
             store(added[n][0])

@@ -22,6 +22,7 @@ P = 128
 PACK = 4
 K_PASS = P * PACK
 HALF = 512
+QUARTER = 256
 TILES = N // P
 
 
@@ -96,21 +97,17 @@ def tile_list_embg_qf_res_kernel(tc, dy, w8, w4_words, w4_scales, res, wgo, offs
             cols = slice(c0, c0 + grouped.shape[1] // PACK)
             nc.vector.quantize_mx(out=dy_codes[a, h][:, cols].bitcast(E5M2), scales=dy_plane[a, h][:, cols], in_=grouped[:])
 
-        def product(i, h, bank):
-            acc = psum.tile([P, HALF], F32, name="acc", tag=bank)
+        def product(i, h, bank, cols=slice(0, HALF)):
+            acc = psum.tile([P, cols.stop - cols.start], F32, name="acc", tag=bank)
             codes, plane = w8_of[i]
             nc.tensor.matmul_mx(
                 out=acc[:], lhsT=codes.bitcast(E4M3), lhsT_scale=plane,
-                rhs=dy_codes[0, h].bitcast(E5M2), rhs_scale=dy_plane[0, h], start=True, stop=False,
+                rhs=dy_codes[0, h][:, cols].bitcast(E5M2), rhs_scale=dy_plane[0, h][:, cols], start=True, stop=False,
             )
-            step = HALF // 2 if (i, h) == (0, 0) else HALF
-            for c in range(0, HALF, step):
-                nc.tensor.matmul_mx(
-                    out=acc[:, c : c + step],
-                    lhsT=w4_codes[:, 2 * P * i : 2 * P * (i + 1)].bitcast(E2M1), lhsT_scale=w4_plane[:, P * i : P * (i + 1)],
-                    rhs=dy_codes[1, h][:, c : c + step].bitcast(E5M2), rhs_scale=dy_plane[1, h][:, c : c + step],
-                    start=False, stop=(c + step == HALF),
-                )
+            nc.tensor.matmul_mx(
+                out=acc[:], lhsT=w4_codes[:, 2 * P * i : 2 * P * (i + 1)].bitcast(E2M1), lhsT_scale=w4_plane[:, P * i : P * (i + 1)],
+                rhs=dy_codes[1, h][:, cols].bitcast(E5M2), rhs_scale=dy_plane[1, h][:, cols], start=False, stop=True,
+            )
             return acc
 
         def sum_on_vector(i, bank):
@@ -140,11 +137,24 @@ def tile_list_embg_qf_res_kernel(tc, dy, w8, w4_words, w4_scales, res, wgo, offs
             sums[i, h] = res_of[i, h]
             nc.scalar.copy(out=sums[i, h], in_=back[:])
 
-        def place(i, h):
+        def scatter(i, c0, c1, values):
             nc.vector.tensor_tensor(
-                out=windows[i][:].indirect(offsets[:, h * HALF // 16 : (h + 1) * HALF // 16]),
-                in0=sums[i, h], in1=weight[:, h * HALF : (h + 1) * HALF], op=MULT,
+                out=windows[i][:].indirect(offsets[:, c0 // 16 : c1 // 16]), in0=values, in1=weight[:, c0:c1], op=MULT
             )
+
+        def place(i, h):
+            scatter(i, h * HALF, (h + 1) * HALF, sums[i, h])
+
+        def load_quarter(name, src, c0):
+            raw = keep.tile([P, QUARTER], F32, name=name, align_bytes=64)
+            nc.sync.dma_start(out=raw[:], in_=src[0:P, c0 : c0 + QUARTER])
+            return raw
+
+        def quarter_sum(q, residual, bank):
+            acc = product(0, 0, bank, slice(q * QUARTER, (q + 1) * QUARTER))
+            total = keep.tile([P, QUARTER], F32, name="sum_q%d" % q, align_bytes=64)
+            nc.vector.tensor_tensor(out=total[:], in0=acc[:], in1=residual[:], op=ADD)
+            return total
 
         def store(i):
             nc.sync.dma_start(out=out[i * P : (i + 1) * P, :], in_=windows[i][:])
@@ -168,15 +178,17 @@ def tile_list_embg_qf_res_kernel(tc, dy, w8, w4_words, w4_scales, res, wgo, offs
         raw_w0 = load_rows("raw_w0", w8[:, 0:P])
         raw_10a = load_rows("raw_10a", dy[K_PASS:K, 0:256])
         raw_10b = load_rows("raw_10b", dy[K_PASS:K, 256:HALF])
-        raw_w1 = load_rows("raw_w1", w8[:, P:256])
         load_w4(0, 2)
-        load_res(0, 1, 0, HALF, "window3")
+        res_a = load_quarter("res_a", res, 0)
         nc.sync.dma_start(offsets[:], offs)
-        nc.sync.dma_start(out=weight[:, 0:HALF], in_=wgo[:, 0:HALF])
+        nc.sync.dma_start(out=weight[:, 0:QUARTER], in_=wgo[:, 0:QUARTER])
+        raw_w1 = load_rows("raw_w1", w8[:, P:256])
+        res_b = load_quarter("res_b", res, QUARTER)
+        nc.sync.dma_start(out=weight[:, QUARTER:HALF], in_=wgo[:, QUARTER:HALF])
         raw_w23 = load_rows("raw_w23", w8[:, 256:512])
         load_w4(2, 2)
         load_res(1, 1, 0, HALF)
-        load_res(3, 1, 0, HALF)
+        load_res(3, 1, 0, HALF, "window6")
         raw_w45 = load_rows("raw_w45", w8[:, 512:768])
         load_w4(4, 4)
         load_res(2, 1, 0, HALF)
@@ -203,7 +215,6 @@ def tile_list_embg_qf_res_kernel(tc, dy, w8, w4_words, w4_scales, res, wgo, offs
         quantize_w8("w0", interleave("scalar", "g_w0", [raw_w0], P), 0)
         quantize_dy(interleave("scalar", "g_10a", [raw_10a], 256), 1, 0, 0)
         quantize_dy(shared("g_10b", raw_10b), 1, 0, 256)
-        quantize_w8("w1", interleave("scalar", "g_w1", [raw_w1], P), 1)
 
         added = [(i, 0) for i in range(3, TILES)] + [(i, 1) for i in range(TILES)]
         turn_bank = ["bank%d" % b for b in (2, 4, 6, 0, 2)] + ["bank%d" % (4, 6, 0)[i % 3] for i in range(TILES)]
@@ -219,22 +230,24 @@ def tile_list_embg_qf_res_kernel(tc, dy, w8, w4_words, w4_scales, res, wgo, offs
         def back(n):
             turn_back(*added[n], back_bank[n])
 
-        sum_on_vector(0, "bank0")
-        place(0, 0)
-        clear_window(nc.gpsimd, 3)
+        scatter(0, 0, QUARTER, quarter_sum(0, res_a, "bank0")[:])
+        second = quarter_sum(1, res_b, "bank4")
+        quantize_w8("w1", interleave("scalar", "g_w1", [raw_w1], P, "window3"), 1)
+        scatter(0, QUARTER, HALF, second[:])
         sum_on_vector(1, "bank1")
-        quantize_w8("w23", interleave("scalar", "g_w23", [raw_w23], 256, "window4"), 2)
+        quantize_w8("w23", interleave("scalar", "g_w23", [raw_w23], 256, "window3"), 2)
         place(1, 0)
-        clear_window(nc.gpsimd, 4)
+        clear_window(nc.gpsimd, 3)
         multiply(0)
         sum_on_vector(2, "bank1")
         turn(0)
-        quantize_w8("w45", interleave("scalar", "g_w45", [raw_w45], 256, "window5"), 4)
+        quantize_w8("w45", interleave("scalar", "g_w45", [raw_w45], 256, "window4"), 4)
         place(2, 0)
-        clear_window(nc.gpsimd, 5)
+        clear_window(nc.gpsimd, 4)
         back(0)
-        quantize_w8("w67", interleave("scalar", "g_w67", [raw_w67], 256, "window6"), 6)
+        quantize_w8("w67", interleave("scalar", "g_w67", [raw_w67], 256, "window5"), 6)
         place(3, 0)
+        clear_window(nc.gpsimd, 5)
         clear_window(nc.gpsimd, 6)
         multiply(1)
         multiply(2)

@@ -167,7 +167,6 @@ def tile_list_embg_qf_res_kernel(tc, dy, w8, w4_words, w4_scales, res, wgo, offs
         make_identity(nc, ident[:])
         clear_window(nc.vector, 0)
         clear_window(nc.vector, 1)
-        clear_window(nc.gpsimd, 2)
 
         raw_00 = load_rows("raw_00", dy[0:K_PASS, 0:HALF])
         staged = keep.tile([P, N // 4], I32, name="staged")
@@ -202,7 +201,7 @@ def tile_list_embg_qf_res_kernel(tc, dy, w8, w4_words, w4_scales, res, wgo, offs
             load_res(i, 2, HALF, J)
 
         def shared(name, raw):
-            grouped = keep.tile([P, 256 * PACK], BF16, name=name, tag=name, align_bytes=64)
+            grouped = keep.tile([P, 256 * PACK], BF16, name=name, tag="window2", align_bytes=64)
             for engine, c0, c1 in ((nc.scalar.copy, 160, 256), (nc.vector.tensor_copy, 0, 160)):
                 engine(
                     out=grouped[:, c0 * PACK : c1 * PACK].rearrange("p (c i t) -> p c t i", i=4, t=PACK),
@@ -215,6 +214,7 @@ def tile_list_embg_qf_res_kernel(tc, dy, w8, w4_words, w4_scales, res, wgo, offs
         quantize_w8("w0", interleave("scalar", "g_w0", [raw_w0], P), 0)
         quantize_dy(interleave("scalar", "g_10a", [raw_10a], 256), 1, 0, 0)
         quantize_dy(shared("g_10b", raw_10b), 1, 0, 256)
+        clear_window(nc.gpsimd, 2)
 
         added = [(i, 0) for i in range(3, TILES)] + [(i, 1) for i in range(TILES)]
         turn_bank = ["bank%d" % b for b in (2, 4, 6, 0, 2)] + ["bank%d" % (4, 6, 0)[i % 3] for i in range(TILES)]

@@ -54,8 +54,8 @@ def tile_list_embg_qf_res_kernel(tc, dy, w8, w4_words, w4_scales, res, wgo, offs
             windows[i] = keep.tile([P, T], F32, name="window%d" % i, tag="window%d" % i, align_bytes=64)
             engine.memset(windows[i][:].bitcast(I32), 0)
 
-        def load_rows(name, rows):
-            raw = keep.tile([P, PACK, rows.shape[1]], F32, name=name, tag=name, align_bytes=64)
+        def load_rows(name, rows, tag=None):
+            raw = keep.tile([P, PACK, rows.shape[1]], F32, name=name, tag=tag or name, align_bytes=64)
             nc.sync.dma_start(out=raw[:], in_=rows.rearrange("(p t) c -> p t c", t=PACK))
             return raw
 
@@ -97,28 +97,32 @@ def tile_list_embg_qf_res_kernel(tc, dy, w8, w4_words, w4_scales, res, wgo, offs
             cols = slice(c0, c0 + grouped.shape[1] // PACK)
             nc.vector.quantize_mx(out=dy_codes[a, h][:, cols].bitcast(E5M2), scales=dy_plane[a, h][:, cols], in_=grouped[:])
 
-        def product(i, h, bank, cols=slice(0, HALF)):
+        def product(i, h, bank, cols=slice(0, HALF), order=(0, 1)):
             acc = psum.tile([P, cols.stop - cols.start], F32, name="acc", tag=bank)
-            codes, plane = w8_of[i]
-            nc.tensor.matmul_mx(
-                out=acc[:], lhsT=codes.bitcast(E4M3), lhsT_scale=plane,
-                rhs=dy_codes[0, h][:, cols].bitcast(E5M2), rhs_scale=dy_plane[0, h][:, cols], start=True, stop=False,
+            weights = (
+                (w8_of[i][0].bitcast(E4M3), w8_of[i][1]),
+                (w4_codes[:, 2 * P * i : 2 * P * (i + 1)].bitcast(E2M1), w4_plane[:, P * i : P * (i + 1)]),
             )
-            nc.tensor.matmul_mx(
-                out=acc[:], lhsT=w4_codes[:, 2 * P * i : 2 * P * (i + 1)].bitcast(E2M1), lhsT_scale=w4_plane[:, P * i : P * (i + 1)],
-                rhs=dy_codes[1, h][:, cols].bitcast(E5M2), rhs_scale=dy_plane[1, h][:, cols], start=False, stop=True,
-            )
+            for a in order:
+                nc.tensor.matmul_mx(
+                    out=acc[:], lhsT=weights[a][0], lhsT_scale=weights[a][1],
+                    rhs=dy_codes[a, h][:, cols].bitcast(E5M2), rhs_scale=dy_plane[a, h][:, cols], start=(a == order[0]), stop=(a == order[1]),
+                )
             return acc
 
-        def sum_on_vector(i, bank):
-            acc = product(i, 0, bank)
-            sums[i, 0] = keep.tile([P, HALF], F32, name="sum_%d" % i, align_bytes=64)[:]
+        def empty(dst, bank):
+            for c in (0, QUARTER):
+                nc.scalar.copy(out=dst[:, c : c + QUARTER], in_=bank[:, c : c + QUARTER])
+
+        def sum_on_vector(i, bank, tag):
+            acc = product(i, 0, bank, order=(1, 0))
+            sums[i, 0] = keep.tile([P, HALF], F32, name="sum_%d" % i, tag=tag, align_bytes=64)[:]
             nc.vector.tensor_tensor(out=sums[i, 0], in0=acc[:], in1=res_of[i, 0], op=ADD)
 
         def product_to_sbuf(i, h, bank):
-            acc = product(i, h, bank)
+            acc = product(i, h, bank, order=(1 - h, h))
             dx_of[i, h] = keep.tile([P, HALF], F32, name="dx_%d_%d" % (i, h), align_bytes=64)
-            nc.scalar.copy(out=dx_of[i, h][:], in_=acc[:])
+            empty(dx_of[i, h], acc)
 
         blocks = [slice(b * P, (b + 1) * P) for b in range(HALF // P)]
 
@@ -128,13 +132,13 @@ def tile_list_embg_qf_res_kernel(tc, dy, w8, w4_words, w4_scales, res, wgo, offs
                 nc.tensor.matmul(turned[:, cols], res_of[i, h][:, cols], ident[:], start=(b == 0), stop=False, is_transpose=True)
             for b, cols in enumerate(blocks):
                 nc.tensor.matmul(turned[:, cols], dx_of[i, h][:, cols], ident[:], start=False, stop=(b == len(blocks) - 1), is_transpose=True)
-            nc.scalar.copy(out=dx_of[i, h][:], in_=turned[:])
+            empty(dx_of[i, h], turned)
 
-        def turn_back(i, h, bank):
+        def turn_back(i, h, bank, tag):
             back = psum.tile([P, HALF], F32, name="back", tag=bank)
             for cols in blocks:
                 nc.tensor.transpose(back[:, cols], dx_of[i, h][:, cols], ident[:])
-            sums[i, h] = res_of[i, h]
+            sums[i, h] = keep.tile([P, HALF], F32, name="sum_%d" % i, tag=tag, align_bytes=64)[:] if tag else res_of[i, h]
             nc.scalar.copy(out=sums[i, h], in_=back[:])
 
         def scatter(i, c0, c1, values):
@@ -187,11 +191,11 @@ def tile_list_embg_qf_res_kernel(tc, dy, w8, w4_words, w4_scales, res, wgo, offs
         raw_w23 = load_rows("raw_w23", w8[:, 256:512])
         load_w4(2, 2)
         load_res(1, 1, 0, HALF)
-        load_res(3, 1, 0, HALF, "window6")
+        load_res(3, 1, 0, HALF)
         raw_w45 = load_rows("raw_w45", w8[:, 512:768])
         load_w4(4, 4)
         load_res(2, 1, 0, HALF)
-        raw_w67 = load_rows("raw_w67", w8[:, 768:N])
+        raw_w67 = load_rows("raw_w67", w8[:, 768:N], "window6")
         load_res(4, 2, 0, HALF)
         raw_01 = load_rows("raw_01", dy[0:K_PASS, HALF:J])
         raw_11 = load_rows("raw_11", dy[K_PASS:K, HALF:J])
@@ -228,18 +232,18 @@ def tile_list_embg_qf_res_kernel(tc, dy, w8, w4_words, w4_scales, res, wgo, offs
             turn_and_add(*added[n], turn_bank[n])
 
         def back(n):
-            turn_back(*added[n], back_bank[n])
+            turn_back(*added[n], back_bank[n], {(3, 0): "window6", (6, 0): "raw_11"}.get(added[n]))
 
         scatter(0, 0, QUARTER, quarter_sum(0, res_a, "bank0")[:])
         second = quarter_sum(1, res_b, "bank4")
         quantize_w8("w1", interleave("scalar", "g_w1", [raw_w1], P, "window3"), 1)
         scatter(0, QUARTER, HALF, second[:])
-        sum_on_vector(1, "bank1")
+        sum_on_vector(1, "bank1", "raw_w23")
         quantize_w8("w23", interleave("scalar", "g_w23", [raw_w23], 256, "window3"), 2)
         place(1, 0)
         clear_window(nc.gpsimd, 3)
         multiply(0)
-        sum_on_vector(2, "bank1")
+        sum_on_vector(2, "bank1", "raw_w45")
         turn(0)
         quantize_w8("w45", interleave("scalar", "g_w45", [raw_w45], 256, "window4"), 4)
         place(2, 0)

@@ -150,13 +150,13 @@ def tile_list_embg_qf_res_kernel(tc, dy, w8, w4_words, w4_scales, res, wgo, offs
             scatter(i, h * HALF, (h + 1) * HALF, sums[i, h])
 
         def load_quarter(name, src, c0):
-            raw = keep.tile([P, QUARTER], F32, name=name, align_bytes=64)
+            raw = keep.tile([P, QUARTER], F32, name=name, tag=name, align_bytes=64)
             nc.sync.dma_start(out=raw[:], in_=src[0:P, c0 : c0 + QUARTER])
             return raw
 
         def quarter_sum(q, residual, bank):
             acc = product(0, 0, bank, slice(q * QUARTER, (q + 1) * QUARTER))
-            total = keep.tile([P, QUARTER], F32, name="sum_q%d" % q, align_bytes=64)
+            total = keep.tile([P, QUARTER], F32, name="sum_q%d" % q, tag=("sum_q0", "window4")[q], align_bytes=64)
             nc.vector.tensor_tensor(out=total[:], in0=acc[:], in1=residual[:], op=ADD)
             return total
 
@@ -171,6 +171,7 @@ def tile_list_embg_qf_res_kernel(tc, dy, w8, w4_words, w4_scales, res, wgo, offs
         make_identity(nc, ident[:])
         clear_window(nc.vector, 0)
         clear_window(nc.vector, 1)
+        clear_window(nc.gpsimd, 2)
 
         raw_00 = load_rows("raw_00", dy[0:K_PASS, 0:HALF])
         staged = keep.tile([P, N // 4], I32, name="staged")
@@ -180,17 +181,16 @@ def tile_list_embg_qf_res_kernel(tc, dy, w8, w4_words, w4_scales, res, wgo, offs
             nc.vector.tensor_copy(out=w4_plane[:].bitcast(I32)[rows, :], in_=staged[rows, :])
         raw_w0 = load_rows("raw_w0", w8[:, 0:P])
         raw_10a = load_rows("raw_10a", dy[K_PASS:K, 0:256])
-        raw_10b = load_rows("raw_10b", dy[K_PASS:K, 256:HALF])
         load_w4(0, 2)
+        raw_10b = load_rows("raw_10b", dy[K_PASS:K, 256:HALF])
         res_a = load_quarter("res_a", res, 0)
         nc.sync.dma_start(offsets[:], offs)
-        nc.sync.dma_start(out=weight[:, 0:QUARTER], in_=wgo[:, 0:QUARTER])
+        nc.sync.dma_start(out=weight[:, 0:HALF], in_=wgo[:, 0:HALF])
         raw_w1 = load_rows("raw_w1", w8[:, P:256])
-        res_b = load_quarter("res_b", res, QUARTER)
-        nc.sync.dma_start(out=weight[:, QUARTER:HALF], in_=wgo[:, QUARTER:HALF])
+        res_b = load_quarter("window3", res, QUARTER)
         raw_w23 = load_rows("raw_w23", w8[:, 256:512])
-        load_w4(2, 2)
         load_res(1, 1, 0, HALF)
+        load_w4(2, 2)
         load_res(3, 1, 0, HALF)
         raw_w45 = load_rows("raw_w45", w8[:, 512:768])
         load_w4(4, 4)
@@ -205,7 +205,7 @@ def tile_list_embg_qf_res_kernel(tc, dy, w8, w4_words, w4_scales, res, wgo, offs
             load_res(i, 2, HALF, J)
 
         def shared(name, raw):
-            grouped = keep.tile([P, 256 * PACK], BF16, name=name, tag="window2", align_bytes=64)
+            grouped = keep.tile([P, 256 * PACK], BF16, name=name, tag="g_dy1", align_bytes=64)
             for engine, c0, c1 in ((nc.scalar.copy, 160, 256), (nc.vector.tensor_copy, 0, 160)):
                 engine(
                     out=grouped[:, c0 * PACK : c1 * PACK].rearrange("p (c i t) -> p c t i", i=4, t=PACK),
@@ -216,9 +216,10 @@ def tile_list_embg_qf_res_kernel(tc, dy, w8, w4_words, w4_scales, res, wgo, offs
         quantize_dy(interleave("scalar", "g_00a", [raw_00[:, :, 0:256]], 256), 0, 0, 0)
         quantize_dy(interleave("vector", "g_00b", [raw_00[:, :, 256:HALF]], 256), 0, 0, 256)
         quantize_w8("w0", interleave("scalar", "g_w0", [raw_w0], P), 0)
-        quantize_dy(interleave("scalar", "g_10a", [raw_10a], 256), 1, 0, 0)
-        quantize_dy(shared("g_10b", raw_10b), 1, 0, 256)
-        clear_window(nc.gpsimd, 2)
+        quantize_dy(shared("g_10a", raw_10a), 1, 0, 0)
+        g_10b = shared("g_10b", raw_10b)
+        first = quarter_sum(0, res_a, "bank0")
+        quantize_dy(g_10b, 1, 0, 256)
 
         added = [(i, 0) for i in range(3, TILES)] + [(i, 1) for i in range(TILES)]
         turn_bank = ["bank%d" % b for b in (2, 4, 6, 0, 2)] + ["bank%d" % (4, 6, 0)[i % 3] for i in range(TILES)]
@@ -234,11 +235,11 @@ def tile_list_embg_qf_res_kernel(tc, dy, w8, w4_words, w4_scales, res, wgo, offs
         def back(n):
             turn_back(*added[n], back_bank[n], {(3, 0): "window6", (6, 0): "raw_11"}.get(added[n]))
 
-        scatter(0, 0, QUARTER, quarter_sum(0, res_a, "bank0")[:])
+        scatter(0, 0, QUARTER, first[:])
         second = quarter_sum(1, res_b, "bank4")
-        quantize_w8("w1", interleave("scalar", "g_w1", [raw_w1], P, "window3"), 1)
+        quantize_w8("w1", interleave("scalar", "g_w1", [raw_w1], P), 1)
         scatter(0, QUARTER, HALF, second[:])
-        sum_on_vector(1, "bank1", "raw_w23")
+        sum_on_vector(1, "bank1", "sum_1")
         quantize_w8("w23", interleave("scalar", "g_w23", [raw_w23], 256, "window3"), 2)
         place(1, 0)
         clear_window(nc.gpsimd, 3)

@@ -121,7 +121,7 @@ def tile_list_embg_qf_res_kernel(tc, dy, w8, w4_words, w4_scales, res, wgo, offs
 
         def product_to_sbuf(i, h, bank):
             acc = product(i, h, bank, order=(1 - h, h))
-            dx_of[i, h] = keep.tile([P, HALF], F32, name="dx_%d_%d" % (i, h), align_bytes=64)
+            dx_of[i, h] = keep.tile([P, HALF], F32, name="dx_%d_%d" % (i, h), tag="window6" if (i, h) == (4, 0) else "dx_%d_%d" % (i, h), align_bytes=64)
             empty(dx_of[i, h], acc)
 
         blocks = [slice(b * P, (b + 1) * P) for b in range(HALF // P)]
@@ -156,7 +156,7 @@ def tile_list_embg_qf_res_kernel(tc, dy, w8, w4_words, w4_scales, res, wgo, offs
 
         def quarter_sum(q, residual, bank):
             acc = product(0, 0, bank, slice(q * QUARTER, (q + 1) * QUARTER))
-            total = keep.tile([P, QUARTER], F32, name="sum_q%d" % q, tag=("sum_q0", "window4")[q], align_bytes=64)
+            total = keep.tile([P, QUARTER], F32, name="sum_q%d" % q, tag=("sum_q0", "window3")[q], align_bytes=64)
             nc.vector.tensor_tensor(out=total[:], in0=acc[:], in1=residual[:], op=ADD)
             return total
 
@@ -171,7 +171,6 @@ def tile_list_embg_qf_res_kernel(tc, dy, w8, w4_words, w4_scales, res, wgo, offs
         make_identity(nc, ident[:])
         clear_window(nc.vector, 0)
         clear_window(nc.vector, 1)
-        clear_window(nc.gpsimd, 2)
 
         raw_00 = load_rows("raw_00", dy[0:K_PASS, 0:HALF])
         staged = keep.tile([P, N // 4], I32, name="staged")
@@ -187,7 +186,7 @@ def tile_list_embg_qf_res_kernel(tc, dy, w8, w4_words, w4_scales, res, wgo, offs
         nc.sync.dma_start(offsets[:], offs)
         nc.sync.dma_start(out=weight[:, 0:HALF], in_=wgo[:, 0:HALF])
         raw_w1 = load_rows("raw_w1", w8[:, P:256])
-        res_b = load_quarter("window3", res, QUARTER)
+        res_b = load_quarter("window2", res, QUARTER)
         raw_w23 = load_rows("raw_w23", w8[:, 256:512])
         load_res(1, 1, 0, HALF)
         load_w4(2, 2)
@@ -195,7 +194,7 @@ def tile_list_embg_qf_res_kernel(tc, dy, w8, w4_words, w4_scales, res, wgo, offs
         raw_w45 = load_rows("raw_w45", w8[:, 512:768])
         load_w4(4, 4)
         load_res(2, 1, 0, HALF)
-        raw_w67 = load_rows("raw_w67", w8[:, 768:N], "window6")
+        raw_w67 = load_rows("raw_w67", w8[:, 768:N], "window5")
         load_res(4, 2, 0, HALF)
         raw_01 = load_rows("raw_01", dy[0:K_PASS, HALF:J])
         raw_11 = load_rows("raw_11", dy[K_PASS:K, HALF:J])
@@ -233,33 +232,34 @@ def tile_list_embg_qf_res_kernel(tc, dy, w8, w4_words, w4_scales, res, wgo, offs
             turn_and_add(*added[n], turn_bank[n])
 
         def back(n):
-            turn_back(*added[n], back_bank[n], {(3, 0): "window6", (6, 0): "raw_11"}.get(added[n]))
+            turn_back(*added[n], back_bank[n], {(3, 0): "window5", (6, 0): "raw_11"}.get(added[n]))
 
         scatter(0, 0, QUARTER, first[:])
         second = quarter_sum(1, res_b, "bank4")
         quantize_w8("w1", interleave("scalar", "g_w1", [raw_w1], P), 1)
         scatter(0, QUARTER, HALF, second[:])
         sum_on_vector(1, "bank1", "sum_1")
-        quantize_w8("w23", interleave("scalar", "g_w23", [raw_w23], 256, "window3"), 2)
+        quantize_w8("w23", interleave("scalar", "g_w23", [raw_w23], 256, "window2"), 2)
         place(1, 0)
-        clear_window(nc.gpsimd, 3)
+        clear_window(nc.gpsimd, 2)
         multiply(0)
         sum_on_vector(2, "bank1", "raw_w45")
         turn(0)
-        quantize_w8("w45", interleave("scalar", "g_w45", [raw_w45], 256, "window4"), 4)
+        quantize_w8("w45", interleave("scalar", "g_w45", [raw_w45], 256, "window3"), 4)
         place(2, 0)
-        clear_window(nc.gpsimd, 4)
+        clear_window(nc.gpsimd, 3)
         back(0)
-        quantize_w8("w67", interleave("scalar", "g_w67", [raw_w67], 256, "window5"), 6)
+        quantize_w8("w67", interleave("scalar", "g_w67", [raw_w67], 256, "window4"), 6)
         place(3, 0)
+        clear_window(nc.gpsimd, 4)
         clear_window(nc.gpsimd, 5)
-        clear_window(nc.gpsimd, 6)
         multiply(1)
         multiply(2)
         for n in (1, 2):
             turn(n)
             back(n)
             place(*added[n])
+        clear_window(nc.gpsimd, 6)
         multiply(3)
         multiply(4)
         late = interleave("scalar", "g_late", [raw_01, raw_11], 256, "window7")

@@ -114,8 +114,8 @@ def tile_list_embg_qf_res_kernel(tc, dy, w8, w4_words, w4_scales, res, wgo, offs
             for c in (0, QUARTER):
                 nc.scalar.copy(out=dst[:, c : c + QUARTER], in_=bank[:, c : c + QUARTER])
 
-        def sum_on_vector(i, bank, tag):
-            acc = product(i, 0, bank, order=(1, 0))
+        def sum_on_vector(i, bank, tag, order):
+            acc = product(i, 0, bank, order=order)
             sums[i, 0] = keep.tile([P, HALF], F32, name="sum_%d" % i, tag=tag, align_bytes=64)[:]
             nc.vector.tensor_tensor(out=sums[i, 0], in0=acc[:], in1=res_of[i, 0], op=ADD)
 
@@ -184,9 +184,10 @@ def tile_list_embg_qf_res_kernel(tc, dy, w8, w4_words, w4_scales, res, wgo, offs
         raw_10b = load_rows("raw_10b", dy[K_PASS:K, 256:HALF])
         res_a = load_quarter("res_a", res, 0)
         nc.sync.dma_start(offsets[:], offs)
-        nc.sync.dma_start(out=weight[:, 0:HALF], in_=wgo[:, 0:HALF])
+        nc.sync.dma_start(out=weight[:, 0:QUARTER], in_=wgo[:, 0:QUARTER])
         raw_w1 = load_rows("raw_w1", w8[:, P:256])
-        res_b = load_quarter("window2", res, QUARTER)
+        res_b = load_quarter("res_b", res, QUARTER)
+        nc.sync.dma_start(out=weight[:, QUARTER:HALF], in_=wgo[:, QUARTER:HALF])
         raw_w23 = load_rows("raw_w23", w8[:, 256:512])
         load_res(1, 1, 0, HALF)
         load_w4(2, 2)
@@ -236,14 +237,14 @@ def tile_list_embg_qf_res_kernel(tc, dy, w8, w4_words, w4_scales, res, wgo, offs
 
         scatter(0, 0, QUARTER, first[:])
         second = quarter_sum(1, res_b, "bank4")
-        quantize_w8("w1", interleave("scalar", "g_w1", [raw_w1], P), 1)
+        quantize_w8("w1", interleave("scalar", "g_w1", [raw_w1], P, "window2"), 1)
         scatter(0, QUARTER, HALF, second[:])
-        sum_on_vector(1, "bank1", "sum_1")
+        sum_on_vector(1, "bank1", "sum_1", (0, 1))
         quantize_w8("w23", interleave("scalar", "g_w23", [raw_w23], 256, "window2"), 2)
         place(1, 0)
         clear_window(nc.gpsimd, 2)
         multiply(0)
-        sum_on_vector(2, "bank1", "raw_w45")
+        sum_on_vector(2, "bank1", "raw_w45", (1, 0))
         turn(0)
         quantize_w8("w45", interleave("scalar", "g_w45", [raw_w45], 256, "window3"), 4)
         place(2, 0)

@@ -36,6 +36,15 @@ def tile_list_embg_qf_res_kernel(tc, dy, w8, w4_words, w4_scales, res, wgo, offs
         weight = keep.tile([P, J], F32, name="weight")
         w4_codes = keep.tile([P, 2 * N], U8, name="w4_codes", align_bytes=64)
         w4_plane = keep.tile([P, N], U8, name="w4_plane", align_bytes=64)
+
+        def load_scales(i, count):
+            cols = slice(P * i, P * (i + count))
+            for q in range(4):
+                rows = w4_scales[0, 4 * q : 4 * q + 4, cols].bitcast(I32)
+                nc.sync.dma_start(
+                    out=w4_plane[32 * q : 32 * q + 32, cols].bitcast(I32), in_=rows.unsqueeze(0).to_broadcast([8, 4, rows.shape[1]])
+                )
+
         ident = keep.tile([P, P], F32, name="ident")
         windows = {}
         sums = {}
@@ -167,17 +176,12 @@ def tile_list_embg_qf_res_kernel(tc, dy, w8, w4_words, w4_scales, res, wgo, offs
         dx_of = {}
         w8_of = {}
 
-        nc.vector.memset(w4_plane[:].bitcast(I32), 0)
         make_identity(nc, ident[:])
         clear_window(nc.vector, 0)
         clear_window(nc.vector, 1)
 
         raw_00 = load_rows("raw_00", dy[0:K_PASS, 0:HALF])
-        staged = keep.tile([P, N // 4], I32, name="staged")
-        for q in range(4):
-            rows = slice(32 * q, 32 * q + 4)
-            nc.sync.dma_start(out=staged[rows, :], in_=w4_scales[0, 4 * q : 4 * q + 4, :].bitcast(I32))
-            nc.vector.tensor_copy(out=w4_plane[:].bitcast(I32)[rows, :], in_=staged[rows, :])
+        load_scales(0, 2)
         raw_w0 = load_rows("raw_w0", w8[:, 0:P])
         raw_10a = load_rows("raw_10a", dy[K_PASS:K, 0:256])
         load_w4(0, 2)
@@ -191,6 +195,7 @@ def tile_list_embg_qf_res_kernel(tc, dy, w8, w4_words, w4_scales, res, wgo, offs
         raw_w23 = load_rows("raw_w23", w8[:, 256:512])
         load_res(1, 1, 0, HALF)
         load_w4(2, 2)
+        load_scales(2, 6)
         load_res(3, 1, 0, HALF)
         raw_w45 = load_rows("raw_w45", w8[:, 512:768])
         load_w4(4, 4)

@@ -209,20 +209,26 @@ def tile_list_embg_qf_res_kernel(tc, dy, w8, w4_words, w4_scales, res, wgo, offs
         for i in range(0, TILES, 2):
             load_res(i, 2, HALF, J)
 
-        def shared(name, raw):
-            grouped = keep.tile([P, 256 * PACK], BF16, name=name, tag="g_dy1", align_bytes=64)
-            for engine, c0, c1 in ((nc.scalar.copy, 160, 256), (nc.vector.tensor_copy, 0, 160)):
+        def shared(name, raw, split, tag):
+            width = raw.shape[2]
+            grouped = keep.tile([P, width * PACK], BF16, name=name, tag=tag, align_bytes=64)
+            for engine, c0, c1 in ((nc.scalar.copy, split, width), (nc.vector.tensor_copy, 0, split)):
                 engine(
                     out=grouped[:, c0 * PACK : c1 * PACK].rearrange("p (c i t) -> p c t i", i=4, t=PACK),
                     in_=raw[:, :, c0:c1].rearrange("p t (c i) -> p c t i", i=4),
                 )
             return grouped
 
-        quantize_dy(interleave("scalar", "g_00a", [raw_00[:, :, 0:256]], 256), 0, 0, 0)
-        quantize_dy(interleave("vector", "g_00b", [raw_00[:, :, 256:HALF]], 256), 0, 0, 256)
+        g_00a = interleave("vector", "g_00a", [raw_00[:, :, 0:QUARTER]], QUARTER)
+        g_00b = shared("g_00b", raw_00[:, :, QUARTER:HALF], 96, "g_00b")
+        quantize_dy(g_00a, 0, 0, 0)
+        quantize_dy(g_00b, 0, 0, QUARTER)
         quantize_w8("w0", interleave("scalar", "g_w0", [raw_w0], P), 0)
-        quantize_dy(shared("g_10a", raw_10a), 1, 0, 0)
-        g_10b = shared("g_10b", raw_10b)
+        g_100 = interleave("vector", "g_100", [raw_10a[:, :, 0:P]], P)
+        g_101 = shared("g_101", raw_10a[:, :, P:QUARTER], 32, "g_dy1")
+        quantize_dy(g_100, 1, 0, 0)
+        quantize_dy(g_101, 1, 0, P)
+        g_10b = shared("g_10b", raw_10b, 160, "g_dy1")
         first = quarter_sum(0, res_a, "bank0")
         quantize_dy(g_10b, 1, 0, 256)
 

from contextlib import ExitStack

import concourse.mybir as mybir
from concourse.masks import make_identity

K, N, T, J = 1024, 1024, 2048, 1024
FLOPS = 2 * K * N * J

F32 = mybir.dt.float32
BF16 = mybir.dt.bfloat16
I32 = mybir.dt.int32
U32 = mybir.dt.uint32
U16 = mybir.dt.uint16
U8 = mybir.dt.uint8
E4M3 = mybir.dt.float8_e4m3fn_x4
E5M2 = mybir.dt.float8_e5m2_x4
E2M1 = mybir.dt.float4_e2m1fn_x4
ADD = mybir.AluOpType.add
MULT = mybir.AluOpType.mult

P = 128
PACK = 4
K_PASS = P * PACK
HALF = 512
QUARTER = 256
TILES = N // P


def tile_list_embg_qf_res_kernel(tc, dy, w8, w4_words, w4_scales, res, wgo, offs, out):
    nc = tc.nc
    with ExitStack() as ctx:
        keep = ctx.enter_context(tc.tile_pool(name="keep", bufs=1))
        psum = ctx.enter_context(tc.psum_pool(name="psum", bufs=1))

        offsets = keep.tile([P, J // 16], U16, name="offsets")
        weight = keep.tile([P, J], F32, name="weight")
        w4_codes = keep.tile([P, 2 * N], U8, name="w4_codes", align_bytes=64)
        w4_plane = keep.tile([P, N], U8, name="w4_plane", align_bytes=64)

        def load_scales(i, count):
            cols = slice(P * i, P * (i + count))
            for q in range(4):
                rows = w4_scales[0, 4 * q : 4 * q + 4, cols].bitcast(I32)
                nc.sync.dma_start(
                    out=w4_plane[32 * q : 32 * q + 32, cols].bitcast(I32), in_=rows.unsqueeze(0).to_broadcast([8, 4, rows.shape[1]])
                )

        ident = keep.tile([P, P], F32, name="ident")
        windows = {}
        sums = {}
        dy_codes = {}
        dy_plane = {}
        for a in range(2):
            dy_codes[a, 0] = keep.tile([P, HALF], U32, name="dy_codes%d" % a, align_bytes=64)[:]
            dy_plane[a, 0] = keep.tile([P, HALF], U8, name="dy_plane%d" % a, align_bytes=64)[:]
        late_codes = keep.tile([P, 2 * HALF], U32, name="late_codes", align_bytes=64)
        late_plane = keep.tile([P, 2 * HALF], U8, name="late_plane", align_bytes=64)
        for a in range(2):
            dy_codes[a, 1] = late_codes[:, a * HALF : (a + 1) * HALF]
            dy_plane[a, 1] = late_plane[:, a * HALF : (a + 1) * HALF]

        def clear_window(engine, i):
            windows[i] = keep.tile([P, T], F32, name="window%d" % i, tag="window%d" % i, align_bytes=64)
            engine.memset(windows[i][:].bitcast(I32), 0)

        def load_rows(name, rows, tag=None):
            raw = keep.tile([P, PACK, rows.shape[1]], F32, name=name, tag=tag or name, align_bytes=64)
            nc.sync.dma_start(out=raw[:], in_=rows.rearrange("(p t) c -> p t c", t=PACK))
            return raw

        def load_res(i, count, c0, c1, tag=None):
            raw = keep.tile([P, count, c1 - c0], F32, name="res_%d_%d" % (i, c0), tag=tag or "res_%d_%d" % (i, c0), align_bytes=64)
            nc.sync.dma_start(out=raw[:], in_=res[i * P : (i + count) * P, c0:c1].rearrange("(i p) c -> p i c", p=P))
            for d in range(count):
                for c in range(c0, c1, HALF):
                    res_of[i + d, c // HALF] = raw[:, d, c - c0 : c - c0 + HALF]

        def load_w4(i, count):
            cols = slice(2 * P * i, 2 * P * (i + count))
            nc.sync.dma_start(out=w4_codes[:, cols].bitcast(I32), in_=w4_words[0][:, cols].bitcast(I32))

        def interleave(engine, name, raws, step, tag=None):
            width = sum(raw.shape[2] for raw in raws)
            grouped = keep.tile([P, width * PACK], BF16, name=name, tag=tag or name, align_bytes=64)
            at = 0
            for raw in raws:
                for c in range(0, raw.shape[2], step):
                    dst = grouped[:, at * PACK : (at + step) * PACK].rearrange("p (c i t) -> p c t i", i=4, t=PACK)
                    src = raw[:, :, c : c + step].rearrange("p t (c i) -> p c t i", i=4)
                    at = at + step
                    if engine == "vector":
                        nc.vector.tensor_copy(out=dst, in_=src)
                    else:
                        nc.scalar.copy(out=dst, in_=src)
            return grouped

        def quantize_w8(name, grouped, first_tile, tag=None):
            width = grouped.shape[1] // PACK
            codes = keep.tile([P, width], U32, name=name + "_codes", tag=tag or name + "_codes", align_bytes=64)
            plane = keep.tile([P, width], U8, name=name + "_plane", align_bytes=64)
            nc.vector.quantize_mx(out=codes[:].bitcast(E4M3), scales=plane[:], in_=grouped[:])
            for d in range(width // P):
                w8_of[first_tile + d] = (codes[:, d * P : (d + 1) * P], plane[:, d * P : (d + 1) * P])

        def quantize_dy(grouped, a, h, c0):
            cols = slice(c0, c0 + grouped.shape[1] // PACK)
            nc.vector.quantize_mx(out=dy_codes[a, h][:, cols].bitcast(E5M2), scales=dy_plane[a, h][:, cols], in_=grouped[:])

        def product(i, h, bank, cols=slice(0, HALF), order=(0, 1)):
            acc = psum.tile([P, cols.stop - cols.start], F32, name="acc", tag=bank)
            weights = (
                (w8_of[i][0].bitcast(E4M3), w8_of[i][1]),
                (w4_codes[:, 2 * P * i : 2 * P * (i + 1)].bitcast(E2M1), w4_plane[:, P * i : P * (i + 1)]),
            )
            for a in order:
                nc.tensor.matmul_mx(
                    out=acc[:], lhsT=weights[a][0], lhsT_scale=weights[a][1],
                    rhs=dy_codes[a, h][:, cols].bitcast(E5M2), rhs_scale=dy_plane[a, h][:, cols], start=(a == order[0]), stop=(a == order[1]),
                )
            return acc

        def empty(dst, bank):
            for c in (0, QUARTER):
                nc.scalar.copy(out=dst[:, c : c + QUARTER], in_=bank[:, c : c + QUARTER])

        def sum_on_vector(i, bank, tag, order):
            acc = product(i, 0, bank, order=order)
            sums[i, 0] = keep.tile([P, HALF], F32, name="sum_%d" % i, tag=tag, align_bytes=64)[:]
            nc.vector.tensor_tensor(out=sums[i, 0], in0=acc[:], in1=res_of[i, 0], op=ADD)

        def product_to_sbuf(i, h, bank):
            acc = product(i, h, bank, order=(1 - h, h))
            dx_of[i, h] = keep.tile([P, HALF], F32, name="dx_%d_%d" % (i, h), tag="window6" if (i, h) == (4, 0) else "dx_%d_%d" % (i, h), align_bytes=64)
            empty(dx_of[i, h], acc)

        blocks = [slice(b * P, (b + 1) * P) for b in range(HALF // P)]

        def turn_and_add(i, h, bank):
            turned = psum.tile([P, HALF], F32, name="turned", tag=bank)
            for b, cols in enumerate(blocks):
                nc.tensor.matmul(turned[:, cols], res_of[i, h][:, cols], ident[:], start=(b == 0), stop=False, is_transpose=True)
            for b, cols in enumerate(blocks):
                nc.tensor.matmul(turned[:, cols], dx_of[i, h][:, cols], ident[:], start=False, stop=(b == len(blocks) - 1), is_transpose=True)
            empty(dx_of[i, h], turned)

        def turn_back(i, h, bank, tag):
            back = psum.tile([P, HALF], F32, name="back", tag=bank)
            for cols in blocks:
                nc.tensor.transpose(back[:, cols], dx_of[i, h][:, cols], ident[:])
            sums[i, h] = keep.tile([P, HALF], F32, name="sum_%d" % i, tag=tag, align_bytes=64)[:] if tag else res_of[i, h]
            nc.scalar.copy(out=sums[i, h], in_=back[:])

        def scatter(i, c0, c1, values):
            nc.vector.tensor_tensor(
                out=windows[i][:].indirect(offsets[:, c0 // 16 : c1 // 16]), in0=values, in1=weight[:, c0:c1], op=MULT
            )

        def place(i, h):
            scatter(i, h * HALF, (h + 1) * HALF, sums[i, h])

        def load_quarter(name, src, c0):
            raw = keep.tile([P, QUARTER], F32, name=name, tag=name, align_bytes=64)
            nc.sync.dma_start(out=raw[:], in_=src[0:P, c0 : c0 + QUARTER])
            return raw

        def quarter_sum(q, residual, bank):
            acc = product(0, 0, bank, slice(q * QUARTER, (q + 1) * QUARTER))
            total = keep.tile([P, QUARTER], F32, name="sum_q%d" % q, tag=("sum_q0", "window3")[q], align_bytes=64)
            nc.vector.tensor_tensor(out=total[:], in0=acc[:], in1=residual[:], op=ADD)
            return total

        def store(i):
            nc.sync.dma_start(out=out[i * P : (i + 1) * P, :], in_=windows[i][:])

        res_of = {}
        dx_of = {}
        w8_of = {}

        make_identity(nc, ident[:])
        clear_window(nc.vector, 0)
        clear_window(nc.vector, 1)

        raw_00 = load_rows("raw_00", dy[0:K_PASS, 0:HALF])
        load_scales(0, 2)
        raw_w0 = load_rows("raw_w0", w8[:, 0:P])
        raw_10a = load_rows("raw_10a", dy[K_PASS:K, 0:256])
        load_w4(0, 2)
        raw_10b = load_rows("raw_10b", dy[K_PASS:K, 256:HALF])
        res_a = load_quarter("res_a", res, 0)
        nc.sync.dma_start(offsets[:], offs)
        nc.sync.dma_start(out=weight[:, 0:QUARTER], in_=wgo[:, 0:QUARTER])
        raw_w1 = load_rows("raw_w1", w8[:, P:256])
        res_b = load_quarter("res_b", res, QUARTER)
        nc.sync.dma_start(out=weight[:, QUARTER:HALF], in_=wgo[:, QUARTER:HALF])
        raw_w23 = load_rows("raw_w23", w8[:, 256:512])
        load_res(1, 1, 0, HALF)
        load_w4(2, 2)
        load_scales(2, 6)
        load_res(3, 1, 0, HALF)
        raw_w45 = load_rows("raw_w45", w8[:, 512:768])
        load_w4(4, 4)
        load_res(2, 1, 0, HALF)
        raw_w67 = load_rows("raw_w67", w8[:, 768:N], "window5")
        load_res(4, 2, 0, HALF)
        raw_01 = load_rows("raw_01", dy[0:K_PASS, HALF:J])
        raw_11 = load_rows("raw_11", dy[K_PASS:K, HALF:J])
        load_res(6, 2, 0, HALF)
        nc.sync.dma_start(out=weight[:, HALF:J], in_=wgo[:, HALF:J])
        for i in range(0, TILES, 2):
            load_res(i, 2, HALF, J)

        def shared(name, raw, split, tag):
            width = raw.shape[2]
            grouped = keep.tile([P, width * PACK], BF16, name=name, tag=tag, align_bytes=64)
            for engine, c0, c1 in ((nc.scalar.copy, split, width), (nc.vector.tensor_copy, 0, split)):
                engine(
                    out=grouped[:, c0 * PACK : c1 * PACK].rearrange("p (c i t) -> p c t i", i=4, t=PACK),
                    in_=raw[:, :, c0:c1].rearrange("p t (c i) -> p c t i", i=4),
                )
            return grouped

        g_00a = interleave("vector", "g_00a", [raw_00[:, :, 0:QUARTER]], QUARTER)
        g_00b = shared("g_00b", raw_00[:, :, QUARTER:HALF], 96, "g_00b")
        quantize_dy(g_00a, 0, 0, 0)
        quantize_dy(g_00b, 0, 0, QUARTER)
        quantize_w8("w0", interleave("scalar", "g_w0", [raw_w0], P), 0)
        g_100 = interleave("vector", "g_100", [raw_10a[:, :, 0:P]], P)
        g_101 = shared("g_101", raw_10a[:, :, P:QUARTER], 32, "g_dy1")
        quantize_dy(g_100, 1, 0, 0)
        quantize_dy(g_101, 1, 0, P)
        g_10b = shared("g_10b", raw_10b, 160, "g_dy1")
        first = quarter_sum(0, res_a, "bank0")
        quantize_dy(g_10b, 1, 0, 256)

        added = [(i, 0) for i in range(3, TILES)] + [(i, 1) for i in range(TILES)]
        turn_bank = ["bank%d" % b for b in (2, 4, 6, 0, 2)] + ["bank%d" % (4, 6, 0)[i % 3] for i in range(TILES)]
        back_bank = ["bank%d" % b for b in (3, 5, 7, 1, 3)] + ["bank%d" % (5, 7, 1)[i % 3] for i in range(TILES)]
        product_bank = ["bank%d" % b for b in (0, 2, 3, 6, 7)] + ["bank%d" % (2 + i % 2) for i in range(TILES)]

        def multiply(n):
            product_to_sbuf(*added[n], product_bank[n])

        def turn(n):
            turn_and_add(*added[n], turn_bank[n])

        def back(n):
            turn_back(*added[n], back_bank[n], {(3, 0): "window5", (6, 0): "raw_11"}.get(added[n]))

        scatter(0, 0, QUARTER, first[:])
        second = quarter_sum(1, res_b, "bank4")
        quantize_w8("w1", interleave("scalar", "g_w1", [raw_w1], P, "window2"), 1)
        scatter(0, QUARTER, HALF, second[:])
        sum_on_vector(1, "bank1", "sum_1", (0, 1))
        quantize_w8("w23", interleave("scalar", "g_w23", [raw_w23], 256, "window2"), 2)
        place(1, 0)
        clear_window(nc.gpsimd, 2)
        multiply(0)
        sum_on_vector(2, "bank1", "raw_w45", (1, 0))
        turn(0)
        quantize_w8("w45", interleave("scalar", "g_w45", [raw_w45], 256, "window3"), 4)
        place(2, 0)
        clear_window(nc.gpsimd, 3)
        back(0)
        quantize_w8("w67", interleave("scalar", "g_w67", [raw_w67], 256, "window4"), 6)
        place(3, 0)
        clear_window(nc.gpsimd, 4)
        clear_window(nc.gpsimd, 5)
        multiply(1)
        multiply(2)
        for n in (1, 2):
            turn(n)
            back(n)
            place(*added[n])
        clear_window(nc.gpsimd, 6)
        multiply(3)
        multiply(4)
        late = interleave("scalar", "g_late", [raw_01, raw_11], 256, "window7")
        nc.vector.quantize_mx(out=late_codes[:].bitcast(E5M2), scales=late_plane[:], in_=late[:])
        clear_window(nc.gpsimd, 7)
        for n in (3, 4):
            turn(n)
            back(n)
            place(*added[n])
        multiply(5)
        multiply(6)
        for n in range(5, len(added)):
            turn(n)
            if n + 2 < len(added):
                multiply(n + 2)
            back(n)
            place(*added[n])
            store(added[n][0])
